import numpy as np, ml_dtypes
CORES = [36,164,52,180,100,228,116,244]
N = 8
BF = ml_dtypes.bfloat16
def gentries(a):
    return np.ascontiguousarray(a.reshape(8, 16, -1).transpose(0, 2, 1)).reshape(8, -1)
def gtable(e):
    e = np.asarray(e); return np.ascontiguousarray(e.reshape(8, -1, 16).transpose(0, 2, 1)).reshape(128, -1).astype(np.int32)
R, F, C, D, B = 16384, 4096, 768, 1, 1 << 20
def passing(at, lim):
    a0 = at[:, 0].reshape(8, R); l = lim.reshape(8, 2)
    return (a0 >= l[:, :1]) & (a0 <= l[:, 1:])
def dims(rng, m, w, first=None):
    lo = rng.integers(-(B >> 1), B >> 2, (8, 1)); hi = lo + w[:, None]; z = rng.random((8, R))
    if first is not None: z[np.arange(8), first] = -1
    ok = np.argsort(np.argsort(z, 1), 1) < m[:, None]
    out = np.where(rng.random((8, R)) < 0.5, rng.integers(1 - B, lo, (8, R)), rng.integers(hi + 1, B, (8, R)))
    return lo, hi, ok, np.where(ok, rng.integers(lo, hi + 1, (8, R)), out)
def living(n, z):
    return np.argsort(np.argsort(z, 1), 1) < n[:, None]
def facts(rng, ok, live, p, where, e=1):
    m = np.sum(ok, axis=1)[:, None]; o = np.argsort(~ok, 1, kind="stable")
    bad = rng.random((N, 8, F)) < p; np.put_along_axis(bad, where, True, 1); bad = bad & ~live[:, None]
    k = np.where(bad, R - m, m); j = np.minimum((rng.random((N, 8, F)) ** e * k).astype(np.int64), k - 1)
    return o[np.arange(8)[:, None], j + np.where(bad, m, 0)]
def pack(lo, hi, v, rest, fk, me):
    rest[:, 0] = v
    return {"at": np.ascontiguousarray(rest.reshape(N, D, 16, R).transpose(0, 2, 1, 3)).reshape(N, 16, D * R).astype(np.int32),
            "lim": np.concatenate([lo, hi], 1).reshape(N, 1, 2 * D).astype(np.int32), "fk": np.stack([gtable(x) for x in fk]), "me": me.reshape(N, 1, F).astype(np.int32)}
def whole(rng, *shape):
    return rng.integers(1 - B, B, shape)
def setup_inputs(rng):
    lo, hi, ok, v = dims(rng, rng.integers(R // 4, 3 * R // 4, 8), rng.integers(B >> 6, B >> 2, 8))
    live = living(rng.integers(C // 4, C, N), rng.random((N, F)))
    return pack(lo, hi, v, whole(rng, 8, 16, R), facts(rng, ok, live, 0.15, rng.integers(0, 8, (N, 1, F))), whole(rng, N, F))
def setup_inputs_full(rng):
    lo, hi, ok, v = dims(rng, rng.integers(R // 4, 3 * R // 4, 8), rng.integers(B >> 6, B >> 2, 8))
    n = np.full(N, C); n[rng.integers(0, N)] = 1; z = rng.random((N, F)); z[:, 0] = -1; z[:, -1] = -2
    return pack(lo, hi, v, whole(rng, 8, 16, R), facts(rng, ok, living(n, z), 0.3, rng.integers(0, 8, (N, 1, F))), whole(rng, N, F))
def setup_inputs_ends(rng):
    w = np.where(rng.permutation(8) < 3, 0, rng.integers(1, 1000, 8))
    lo, hi, ok, v = dims(rng, rng.integers(R // 4, 3 * R // 4, 8), w); h = rng.random((8, R)) < 0.5
    v = np.where(ok, np.where(h, lo, hi), np.where(h, lo - 1, hi + 1)); j = np.arange(F)
    live = living(rng.integers(C // 4, C + 1, N), np.minimum(j, F - 1 - j)[None] + np.zeros((N, 1)))
    return pack(lo, hi, v, whole(rng, 8, 16, R), facts(rng, ok, live, 0.1, rng.integers(0, 8, (N, 1, F))), whole(rng, N, F))
def setup_inputs_alike(rng):
    m = np.where(rng.permutation(8) < 4, 1, R - 1)
    lo, hi, ok, v = dims(rng, m, rng.integers(0, B >> 2, 8), np.where(rng.random(8) < 0.5, 0, R - 1))
    live = living(rng.integers(C // 4, C + 1, N), rng.random((N, F))); fk = facts(rng, ok, live, 0.1, rng.integers(0, 8, (N, 1, F)))
    q = rng.integers(0, N); s = np.flatnonzero(live[q]); fk[q][:, s] = fk[q][:, s[:1]]
    return pack(lo, hi, v, whole(rng, 8, 16, R), fk, whole(rng, N, F))
def setup_inputs_near(rng):
    lo, hi, ok, v = dims(rng, rng.integers(R // 4, 3 * R // 4, 8), rng.integers(B >> 6, B >> 2, 8))
    where = np.where(rng.random((N, 1, 1)) < 0.5, rng.integers(0, 8, (N, 1, 1)), rng.integers(0, 8, (N, 1, F)))
    live = living(rng.integers(C // 4, C + 1, N), rng.random((N, F))); sg = rng.choice(np.array([-1, 1]), (1, 16, 1))
    rest = sg * (B - 1 - rng.integers(0, 50, (8, 16, R))); me = rng.choice(np.array([-1, 1]), (N, 1)) * (B - 1 - rng.integers(0, 50, (N, F)))
    return pack(lo, hi, v, rest, facts(rng, ok, live, 0.0, where), me)
def setup_inputs_spread(rng):
    lo, hi, ok, v = dims(rng, np.maximum(1, R >> rng.integers(1, 10, 8)), 1 << rng.integers(0, 18, 8))
    live = living(np.maximum(1, C >> rng.integers(0, 6, N)), rng.random((N, F)))
    rest = whole(rng, 8, 16, R) >> rng.integers(0, 20, (8, 16, R)); me = whole(rng, N, F) >> rng.integers(0, 20, (N, F))
    return pack(lo, hi, v, rest, facts(rng, ok, live, rng.random((1, 8, 1)), rng.integers(0, 8, (N, 1, F)), 4), me)
def check_inputs(d):
    bad = [k for k in ("at", "lim", "me") if not ((d[k] > -B) & (d[k] < B)).all()]
    if not ((d["fk"] >= 0) & (d["fk"] < R)).all(): return bad + ["fk"]
    ok = passing(d["at"], d["lim"]); g = np.arange(8)[:, None]
    n = [int(np.sum(np.all(ok[g, gentries(a)], axis=0))) for a in d["fk"]]
    return bad + ([] if min(n) >= 1 and max(n) <= C else ["survivors"])
def reference(at, lim, fk, me):
    y = np.zeros((N, 16, C + 1), np.int64); ok = passing(at, lim); g = np.arange(8)[:, None]
    a = np.ascontiguousarray(at.reshape(N, 16, D, R).transpose(0, 2, 1, 3)).reshape(8, 16, R).astype(np.int64)
    for r in range(N):
        k = gentries(fk[r]); s = np.flatnonzero(np.all(ok[g, k], axis=0)); n = len(s)
        y[r, :, :n] = me[r, 0][s][None]
        for d in range(8): y[r, :, :n] += a[d][:, k[d, s]]
        y[r, :, C] = n
    return {"y": np.asarray(y, np.float32)}

@@ -1,0 +1,297 @@
+import math
+import numpy as np
+from concourse.bass import DstId, RemoteDMATransfer
+from concourse.mybir import dt, AluOpType, AxisListType, ActivationFunctionType
+
+ALU = AluOpType
+ACT = ActivationFunctionType
+R = 16384
+Z0 = 8
+NH, WH = 3, 2752
+NQ = 4
+QP = WH // NQ
+W0 = 256
+OWN = R - NH * WH - W0
+
+F32, BF, I32, U16 = "float32", "bfloat16", "int32", "uint16"
+SCRATCH = {}
+for _d, _l in ((I32, "x0 128 limi 2 ip 32 ipm 32 isl 10 ism 10 f1 6 f1m 6 f2 6 fv 6 fw 6 fa 6 fb 6 fi 6 fks 256 k1 256 k2 256 "
+                     "k3 256 bb 256 di 256 db 256 t1 128 t2 64 v 512 c8 32 mei 32 met 256"),
+               (BF, "mk 128 ml 128 ones 128 idb 128 tri 128 bi 8 pw0 16 pm 16 pw 16 ow 16 bf 256 pbt 256 sw 2048 ge 4096 pre 32"),
+               (F32, "limf 2 orow 128 ie 16 ec 16 ct 32 on32 32 sl9 10 sl8 8 nm 32 zz 32 aa 32 mef 32 idf 128 wk 2048 "
+                     "zo 240 mey 96 od 672 ld 768 a1 192 a2 96 a4 96 a3 96 b1 96 b2 96 yt 97"),
+               (U16, "fp 6 lk 256 pos 32 ks 48 lt 42 lo 6")):
+    _w = _l.split()
+    for _k in range(0, len(_w), 2):
+        SCRATCH[_w[_k]] = ("sbuf", [128, int(_w[_k + 1])], _d)
+SCRATCH["tw"] = ("sbuf", [128, Z0 + R], I32)
+SCRATCH["ds"] = ("dram", [NQ * NH, 128, QP // 8], I32)
+SCRATCH["hs"] = ("dram", [NQ, 128, QP // 8], I32)
+SCRATCH["ds0"] = ("dram", [128, W0 // 8], I32)
+SCRATCH["hs0"] = ("dram", [128, W0 // 8], I32)
+SCRATCH["dl"] = ("dram", [8, 128, 16], BF)
+for _k in ("psa", "psd0", "psd1", "psm"):
+    SCRATCH[_k] = ("psum", [128, 512], F32)
+SCRATCH["pst"] = ("psum", [128, 1024], BF)
+SEMAPHORES = (["s%d" % k for k in range(125)] + ["hin%d" % k for k in range(NQ)]
+              + ["mi", "h1", "lx", "lw", "h2", "dx", "dw", "h3", "hsm", "hw", "h0", "h00"])
+
+
+def helpers(core, topo):
+    return [c for c in topo.cores_of(core) if c != core and topo.die(c) == topo.die(core)][:NH]
+
+
+def off_chip(core, T, topo):
+    es = [topo.engines(core, c) for c in T.cores if c != core]
+    return [e for e in es[0] if all(e in x for x in es)]
+
+
+def hand_on(g, core, T, topo, owner):
+    S, Y, A = T.sem, g.sync, g.scalar
+    h = helpers(owner, topo).index(core)
+    c0 = Z0 + OWN + W0 + WH * h
+    parts = [(c0 + QP * p, QP, T.hs[p], S["hin%d" % p], 2) for p in range(NQ)]
+    if h == 0:
+        parts = [(Z0 + OWN, W0, T.hs0[:], S.hsm, len(off_chip(owner, T, topo)))] + parts
+    for p, (c, w, src, sem, n) in enumerate(parts):
+        for q in (Y, A):
+            q.wait_ge(sem, n)
+        for u in range(8):
+            (Y, A)[u % 2].dma_start(T.tw[16 * u:16 * u + 16, c:c + w], src).then_inc(S["s%d" % p], 16)
+    rid, pid = topo.addr(owner, core)
+    for p, (c, w, src, sem, n) in enumerate(parts):
+        g.wait_ge(S["s%d" % p], 128)
+        g.remote_dma(T.tw[:, c:c + w], T.tw[:, c:c + w], S.hw, S.h0, pid, rid, topo.mask(core, owner))
+    g.wait_ge(S.h0, len(parts) * len(topo.engines(core, owner)))
+
+
+def rank_program(g, core, T, topo):
+    me = T.rank_of(core)
+    if me is None:
+        for c in T.cores:
+            if core in helpers(c, topo):
+                hand_on(g, core, T, topo, c)
+        return
+    S = T.sem
+    Q = {"g": g, "v": g.vector, "s": g.scalar, "y": g.sync, "t": g.tensor}
+    V, A, P, Y = g.vector, g.scalar, g.tensor, g.sync
+    count, seen, total = [0], {}, {}
+
+    def wait(q, *toks):
+        for name, val in toks:
+            if seen.get((q, name), 0) < val:
+                Q[q].wait_ge(S[name], val)
+                seen[(q, name)] = val
+
+    def do(q, deps, fns, n=1):
+        wait(q, *deps)
+        fns = fns if isinstance(fns, list) else [fns]
+        name = "s%d" % count[0]
+        count[0] += 1
+        for f in fns:
+            f().then_inc(S[name], n)
+        total[name] = n * len(fns)
+        return (name, total[name])
+
+    CORES = list(T.cores)
+    half = me // 4
+    other = [r for r in range(8) if r // 4 != half]
+    mine = [r for r in range(8) if r // 4 == half and r != me]
+    peers = other + mine
+
+    def slot(src, dst):
+        return src % 4 if src // 4 != dst // 4 else 4 + [r for r in range(8) if r // 4 == dst // 4 and r != dst].index(src)
+
+    def at_core(c):
+        rid, pid = topo.addr(c, core)
+        return DstId(rid=rid, pnc=pid)
+
+    def dest(r):
+        return at_core(CORES[r])
+    eng = off_chip(core, T, topo)
+    ln2 = math.log(2.0)
+
+    hp = helpers(core, topo)
+    t_lim = do("s", [], lambda: A.dma_start(T.limi[0:1, :], T.lim[:]), 16)
+    t_x0 = do("y", [], lambda: Y.dma_start(T.x0[:], T.at[0:1, :]), 16)
+    t_ds0 = do("y", [], lambda: Y.dma_start(T.ds0[:], T.at[:, OWN:OWN + W0]), 16)
+    t_fk = do("s", [], lambda: A.dma_start(T.fks[:], T.fk[:]), 16)
+    t_mei = do("s", [], lambda: A.dma_start(T.mei[:], T.me[:]), 16)
+    s0 = OWN + W0
+
+    def strip(p):
+        return do("y", [], [lambda h=h, k=k: Y.dma_start(
+            T.ds[NQ * h + k], T.at[:, s0 + WH * h + QP * k:s0 + WH * h + QP * k + QP]) for k in (2 * p, 2 * p + 1) for h in range(NH)], 16)
+    t_ds = [strip(0)]
+    t_vf = do("y", [], lambda: Y.dma_start(T.v[:], T.at[0:4, :]), 16)
+    t_ds.append(strip(1))
+
+    t_ie = do("g", [], lambda: g.iota(T.ie[:], [[-8, 16]], 0, 1, allow_small_or_imprecise_dtypes=True))
+    t_is = do("g", [], lambda: g.iota(T.isl[:], [[-1, 10]], 128, 1))
+    t_ip = do("g", [], lambda: g.iota(T.ip[:], [[1, 32]], 0, 32))
+    t_c8 = do("v", [], [lambda: V.memset(T.c8[:], Z0), lambda: V.memset(T.tw[:, 0:Z0], 0)])
+    t_or = do("v", [], lambda: V.memset(T.orow[0:1, :], 1.0))
+    t_ones = do("v", [], lambda: V.memset(T.ones[:], 1.0))
+    t_pw0 = do("s", [t_ie], lambda: A.activation(T.pw0[:], T.ie[:], ACT.Exp, bias=7 * ln2, scale=-ln2))
+    t_ec = do("v", [t_ie], lambda: V.tensor_scalar(T.ec[:], T.ie[:], 7.0, 0.0, ALU.min, ALU.max))
+    t_id = do("g", [t_ones], lambda: g.affine_select(T.idb[:], T.ones[:], [[1, 128]], ALU.is_equal, 0.0, 0, -1))
+    t_sw = [do("v", [], lambda: V.memset(T.sw[:, 0:1024], 0.0))]
+    t_pm = do("v", [t_ec], lambda: V.tensor_tensor(T.pm[:], T.ie[:], T.ec[:], ALU.is_equal))
+    t_ism = do("v", [t_is], lambda: V.tensor_scalar(T.ism[:], T.isl[:], 15, None, ALU.bitwise_and))
+    t_ipm = do("v", [t_ip], lambda: V.tensor_scalar(T.ipm[:], T.ip[:], 511, None, ALU.bitwise_and))
+    t_sl9 = do("v", [t_ism], lambda: V.tensor_scalar(T.sl9[:], T.ism[:], 0.0, None, ALU.is_equal))
+    t_ct = do("v", [t_ipm], lambda: V.tensor_scalar(T.ct[:], T.ipm[:], 769.0, None, ALU.add))
+
+    wait("g", t_ds0)
+    rid, pid = topo.addr(hp[0], core)
+    g.remote_dma(T.hs0[:], T.ds0[:], S.hsm, S.h00, pid, rid, sum(1 << e for e in eng))
+
+    t_lf = do("v", [t_lim], lambda: V.tensor_copy(T.limf[0:1, :], T.limi[0:1, :]))
+    t_pl = do("t", [t_or, t_lf], lambda: P.matmul(T.psa[:, 0:2], T.orow[0:1, :], T.limf[0:1, :], True, True))
+    t_sw.append(do("v", [], lambda: V.memset(T.sw[:, 1024:1536], 0.0)))
+    t_ml = do("v", [t_x0, t_pl], [lambda: V.tensor_scalar(T.ml[:], T.x0[:], T.psa[:, 0:1], None, ALU.is_lt),
+                                  lambda: V.tensor_scalar(T.mk[:], T.x0[:], T.psa[:, 1:2], None, ALU.is_gt)])
+    t_pw = do("v", [t_pw0, t_pm], lambda: V.tensor_tensor(T.pw[:], T.pw0[:], T.pm[:], ALU.mult))
+    t_pp = do("t", [t_ml, t_pw], [lambda: P.matmul(T.psa[:, 16:32], T.ml[:], T.pw[:], True, False),
+                                  lambda: P.matmul(T.psa[:, 16:32], T.mk[:], T.pw[:], False, True)])
+    t_k1 = do("v", [t_fk], lambda: V.tensor_scalar(T.k1[:], T.fks[:], 0x3C7F, None, ALU.bitwise_and))
+    t_own = do("v", [t_pp], lambda: V.tensor_copy(T.ow[:], T.psa[:, 16:32]))
+    wait("g", t_own)
+    g.remote_dma_fused([RemoteDMATransfer(dst_ids=[dest(r) for r in peers], dma_engine_mask=sum(1 << e for e in eng),
+                                          remote_sem=S.mi, srcs=[T.ow[:]], dsts=[T.dl[me] for r in peers])], local_sem=S.h1)
+
+    he = topo.engines(core, hp[0])[::-1]
+
+    def strips(p):
+        todo = [(i, c, k) for k in (2 * p, 2 * p + 1) for i, c in enumerate(hp)]
+        g.remote_dma_fused([RemoteDMATransfer(dst_ids=[at_core(c)], dma_engine_mask=(1 << he[2 * j]) | (1 << he[2 * j + 1]),
+                                              remote_sem=S["hin%d" % k], srcs=[T.ds[NQ * i + k]], dsts=[T.hs[k]])
+                            for j, (i, c, k) in enumerate(todo)], local_sem=S.h0)
+    wait("g", t_ds[0])
+    strips(0)
+
+    t_k2 = do("v", [t_k1], lambda: V.tensor_scalar(T.k2[:], T.k1[:], 16.0 + 1.0 / 1024.0, None, ALU.mult))
+    t_bb = do("v", [t_fk], lambda: V.tensor_scalar(T.bb[:], T.fks[:], 7, 7, ALU.arith_shift_right, ALU.bitwise_and))
+    t_sw.append(do("v", [], lambda: V.memset(T.sw[:, 1536:2048], 0.0)))
+    t_k3 = do("v", [t_k2], lambda: V.tensor_scalar(T.k3[:], T.k2[:], 2047, None, ALU.bitwise_and))
+    t_bf = do("v", [t_bb], [lambda c=c: V.tensor_copy(T.bf[:, 128 * c:128 * c + 128], T.bb[:, c::2]) for c in range(2)])
+    t_lk = do("v", [t_k3], [lambda c=c: V.tensor_copy(T.lk[:, 128 * c:128 * c + 128], T.k3[:, c::2]) for c in range(2)])
+    t_mef = do("v", [t_mei], lambda: V.tensor_copy(T.mef[:], T.mei[:]))
+
+    t_on32 = do("s", [t_ones], lambda: A.activation(T.on32[:], T.ones[:, 0:32], ACT.Copy))
+    t_sl8 = do("s", [t_sl9], lambda: A.activation(T.sl8[:], T.sl9[:, 0:8], ACT.Identity, bias=T.sl9[:, 8:9]))
+    t_idf = do("s", [t_id], lambda: A.activation(T.idf[:], T.idb[:], ACT.Copy))
+    t_wkz = do("s", [t_sw[0]], lambda: A.activation(T.wk[:, 0:768], T.sw[:, 0:768], ACT.Copy, scale=0.0))
+    t_bt = do("t", [t_id, t_bf], [lambda c=c: P.transpose(
+        T.pst[:, 128 * c:128 * c + 128], T.bf[:, 128 * c:128 * c + 128], T.idb[:]) for c in range(2)])
+    t_pbt = do("s", [t_bt], lambda: A.activation(T.pbt[:], T.pst[:, 0:256], ACT.Exp, scale=ln2))
+    t_mt = do("t", [t_mef, t_idf], [lambda c=c: P.matmul(
+        T.psm[0:16, c:256:2], T.mef[:, 16 * c:16 * c + 16], T.idf[:], True, True) for c in range(2)])
+
+    t_dl = do("y", [t_own], lambda: Y.dma_start(T.dl[me], T.ow[:]), 16)
+    t_win = do("y", [t_dl, t_wkz, ("mi", 7 * len(eng))] + t_sw, lambda: Y.dma_start(T.sw[0::16, :], T.dl[:]), 16)
+    wait("y", t_vf, t_c8)
+    t_v = do("y", [], [lambda q=q: Y.dma_start(T.v[16 * q:16 * q + 8, :], T.fk[:, 32 * q:32 * q + 32]) for q in range(8)]
+             + [lambda: Y.dma_start(T.v[8::16, :], T.c8[:])], 16)
+
+    t_bi = do("g", [], lambda: g.affine_select(T.bi[:], T.ones[:, 0:8], [[-16, 8]], ALU.is_equal, 0.0, 0, 1))
+    t_tri = do("g", [], lambda: g.affine_select(T.tri[:], T.ones[:], [[1, 128]], ALU.is_gt, 0.0, 0, -1))
+    t_f = do("g", [], [lambda: g.iota(T.f1[:], [[0, 6]], 0, 1), lambda: g.iota(T.f2[:], [[16, 6]], 0, 0)])
+    wait("g", t_win, t_ds[1])
+    strips(1)
+
+    sw = T.sw[:, 0:2048]
+    t_gv, t_gs = [], []
+    for c in range(2):
+        o, l = 2048 * c, 128 * c
+        t_gv.append(do("v", [t_win, t_lk], lambda: V.tensor_copy(T.ge[:, o:o + 1024], sw.indirect(T.lk[:, l:l + 64]))))
+        t_gs.append(do("s", [t_win, t_lk], lambda: A.activation(
+            T.ge[:, o + 1024:o + 2048], sw.indirect(T.lk[:, l + 64:l + 128]), ACT.Copy)))
+        if c == 0:
+            t_met = do("v", [t_mt], lambda: V.tensor_copy(T.met[0:16, :], T.psm[0:16, 0:256]))
+    t_zoz = do("s", [t_gs[0]], lambda: A.activation(T.zo[:], T.ge[:, 1024:1264], ACT.Copy, scale=0.0))
+    t_zo = do("s", [t_zoz, t_sl9], lambda: A.activation(T.zo[:, 112:128], T.zo[:, 0:16], ACT.Identity, bias=T.sl9[:, 9:10]))
+    t_tw = [do("y", [], lambda: Y.dma_start(T.tw[0:16, Z0:Z0 + OWN], T.at[:, 0:OWN]), 16)]
+    t_mr = do("y", [t_met], [lambda q=q: Y.dma_start(T.v[16 * q + 9:16 * q + 10, :], T.met[0:16, 32 * q:32 * q + 32]) for q in range(8)], 16)
+    t_tw.append(do("y", [], [lambda u=u: Y.dma_start(
+        T.tw[16 * u:16 * u + 16, Z0:Z0 + OWN], T.at[:, 0:OWN]) for u in range(1, 8)], 16))
+
+    t_m = []
+    for c in range(2):
+        ps = (T.psd0, T.psd1)[c]
+        o, a, b, e = 128 * c, 64 * c, 32 * c, 16 * c
+        t_d = do("t", [t_bi, t_gv[c], t_gs[c]], [lambda q=q: P.matmul(
+            ps[:, q:128:16], T.ge[:, 2048 * c + q:2048 * c + 2048:16], T.bi[:], True, True) for q in range(16)])
+        t_di = do("v", [t_d, t_pbt], lambda: V.tensor_tensor(T.di[:, o:o + 128], ps[:, 0:128], T.pbt[:, o:o + 128], ALU.mult))
+        t_db = do("v", [t_di], lambda: V.tensor_scalar(
+            T.db[:, o:o + 128], T.di[:, o:o + 128], 7, 1, ALU.logical_shift_right, ALU.bitwise_and))
+        t_1 = do("v", [t_db], lambda: V.tensor_tensor(T.t1[:, a:a + 64], T.db[:, o:o + 64], T.db[:, o + 64:o + 128], ALU.max))
+        t_2 = do("v", [t_1], lambda: V.tensor_tensor(T.t2[:, b:b + 32], T.t1[:, a:a + 32], T.t1[:, a + 32:a + 64], ALU.max))
+        t_m.append(do("v", [t_2], lambda: V.tensor_tensor(T.nm[:, e:e + 16], T.t2[:, b:b + 16], T.t2[:, b + 16:b + 32], ALU.max)))
+
+    t_pre = do("v", [t_on32] + t_m, lambda: V.tensor_tensor_scan(T.pre[:], T.on32[:], T.nm[:], 0.0, ALU.add, ALU.subtract))
+    t_off = do("t", [t_tri, t_ones, t_own, t_pre], [
+        lambda: P.matmul(T.psa[:, 64:65], T.tri[:], T.pre[:, 31:32], True, True),
+        lambda: P.matmul(T.psa[:, 65:66], T.ones[:], T.pre[:, 31:32], True, True)])
+    t_zz = do("v", [t_ct], lambda: V.tensor_tensor(T.zz[:], T.nm[:], T.ct[:], ALU.mult))
+    t_aa = do("v", [t_zz, t_pre], lambda: V.tensor_tensor(T.aa[:], T.pre[:], T.zz[:], ALU.add))
+    t_pos = do("v", [t_aa, t_off], lambda: V.tensor_scalar(T.pos[:], T.aa[:], T.psa[:, 64:65], -1.0, ALU.add, ALU.add))
+
+    wait("v", t_v, t_mr, t_vf)
+    t_wk = t_wkz
+    for c in range(2):
+        t_wk = do("v", [t_pos, t_wk], lambda: V.tensor_copy(T.wk[:, 0:2048].indirect(T.pos[:, 16 * c:16 * c + 16]), T.v[:, c::2]))
+    t_n = do("v", [], lambda: V.tensor_copy(T.yt[:, 96:97], T.psa[:, 65:66]))
+    t_k = do("t", [t_wk, t_sl8, t_pos, t_n], [lambda c=c: P.matmul(
+        T.psa[:, 128 + c:176:6], T.wk[:, c:768:6], T.sl8[:], True, True) for c in range(6)])
+    t_ks = do("v", [t_k], lambda: V.tensor_copy(T.ks[:], T.psa[:, 128:176]))
+    t_lo = do("v", [], lambda: V.tensor_copy(T.lo[:], T.psa[:, 128 + 6 * me:134 + 6 * me]))
+
+    wait("g", t_ks)
+    g.remote_dma_fused([RemoteDMATransfer(
+        dst_ids=[dest(r)], dma_engine_mask=1 << eng[i], remote_sem=S.lx if r in other else S.lw,
+        srcs=[T.ks[:, 6 * r:6 * r + 6]], dsts=[T.lt[:, 6 * slot(me, r):6 * slot(me, r) + 6]]) for i, r in enumerate(peers)], local_sem=S.h2)
+
+    t_me = do("t", [t_wk, t_zo, t_met], [lambda u=u: P.matmul(
+        T.psm[:, 0:96], T.zo[:, 112 - 16 * u:240 - 16 * u], T.wk[:, 96 * u:96 * u + 96], u == 0, u == 7) for u in range(8)])
+    t_mey = do("s", [t_me], lambda: A.activation(T.mey[:], T.psm[:, 0:96], ACT.Copy))
+
+    t_f1m = do("v", [t_f], lambda: V.tensor_scalar(T.f1m[:], T.f1[:], 15, None, ALU.bitwise_and))
+    t_fv = do("v", [t_f1m], lambda: V.tensor_tensor(T.fv[:], T.f1m[:], T.f2[:], ALU.add))
+    t_fw = do("v", [t_fv], [lambda: V.tensor_scalar(T.fw[:], T.fv[:], 1.0 / 6.0, -0.41666, ALU.mult, ALU.add),
+                            lambda: V.tensor_scalar(T.fb[:], T.fv[:], 16.0, None, ALU.mult)])
+    t_fa = do("v", [t_fw], lambda: V.tensor_scalar(T.fa[:], T.fw[:], -95.0, None, ALU.mult))
+    t_fi = do("v", [t_fa], lambda: V.tensor_tensor(T.fi[:], T.fa[:], T.fb[:], ALU.add))
+    t_fp = do("v", [t_fi], lambda: V.tensor_copy(T.fp[:], T.fi[:]))
+
+    win = T.tw[:, 0:Z0 + R]
+    nw = sum((NQ + 1 if i == 0 else NQ) * len(topo.engines(c, core)) for i, c in enumerate(hp))
+    wait("v", *t_tw, t_c8, ("hw", nw), ("lx", 4))
+    t_ox = do("v", [], lambda: V.tensor_copy(T.od[:, 0:384], win.indirect(T.lt[:, 0:24])))
+    wait("v", ("lw", 3))
+    t_ow = do("v", [], lambda: V.tensor_copy(T.od[:, 384:672], win.indirect(T.lt[:, 24:42])))
+    t_oo = do("v", [t_lo], lambda: V.tensor_copy(T.ld[:, 672:768], win.indirect(T.lo[:, 0:6])))
+    for tok, rs, sem in ((t_ox, other, "dx"), (t_ow, mine, "dw")):
+        wait("g", tok)
+        g.remote_dma_fused([RemoteDMATransfer(
+            dst_ids=[dest(r)], dma_engine_mask=(1 << eng[2 * i]) | (1 << eng[2 * i + 1]), remote_sem=S[sem],
+            srcs=[T.od[:, 96 * slot(r, me):96 * slot(r, me) + 96]],
+            dsts=[T.ld[:, 96 * slot(me, r):96 * slot(me, r) + 96]]) for i, r in enumerate(rs)], local_sem=S.h3)
+
+    wait("v", ("dx", 8))
+    t_a1 = do("v", [], lambda: V.tensor_tensor(T.a1[:], T.ld[:, 0:192], T.ld[:, 192:384], ALU.add))
+    t_a2 = do("v", [t_a1], lambda: V.tensor_tensor(T.a2[:], T.a1[:, 0:96], T.a1[:, 96:192], ALU.add))
+    t_a4 = do("v", [t_a2, t_oo], lambda: V.tensor_tensor(T.a4[:], T.a2[:], T.ld[:, 672:768], ALU.add))
+    t_a3 = do("v", [t_a4, t_fp, t_mey], lambda: V.tensor_tensor(T.a3[:], T.a4[:, 0:96].indirect(T.fp[:, 0:6]), T.mey[:], ALU.add))
+    wait("v", ("dw", 6))
+    t_b1 = do("v", [], lambda: V.tensor_tensor(T.b1[:], T.ld[:, 384:480], T.ld[:, 480:576], ALU.add))
+    t_b2 = do("v", [t_a3], lambda: V.tensor_tensor(T.b2[:], T.ld[:, 576:672].indirect(T.fp[:, 0:6]), T.a3[:], ALU.add))
+    t_y = do("v", [t_b1, t_b2], lambda: V.tensor_tensor(T.yt[:, 0:96], T.b1[:, 0:96].indirect(T.fp[:, 0:6]), T.b2[:], ALU.add))
+    done = []
+    for q, us in (("y", range(0, 4)), ("s", range(4, 8))):
+        done.append(do(q, [t_y, t_n], [lambda u=u: Q[q].dma_start(
+            T.y[:, 96 * u:96 * u + (97 if u == 7 else 96)], T.yt[16 * u:16 * u + 16, 0:97 if u == 7 else 96]) for u in us], 16))
+    wait("y", *done)
+    wait("g", ("h1", len(eng)), ("h3", 14), ("h2", 7), ("h0", 8 * NH), ("h00", len(eng)))
+    waited = {name for _, name in seen}
+    wait("g", *[(n, t) for n, t in total.items() if n not in waited])

@@ -5,36 +5,39 @@ from concourse.mybir import dt, AluOpType, AxisListType, ActivationFunctionType
 
 ALU = AluOpType
 ACT = ActivationFunctionType
-R = 16384
-Z0 = 8
-NH, WH = 3, 2752
-NQ = 4
-QP = WH // NQ
-W0 = 256
-OWN = R - NH * WH - W0
+R, BLK = 16384, 2048
+S7 = 7 * BLK
+NH = 3
+W0 = 32
+HOP2 = ((1,), (2, 3), (4, 5, 6, 7))
+HOP3 = ((1,), (2, 3), (4, 5), (6,), (7,))
+WP = ((184, 184, 184), (184, 184, 184))
+C0 = [W0 + sum(sum(w) for w in WP[:k]) for k in range(len(WP) + 1)]
+VG = 24
 
 F32, BF, I32, U16 = "float32", "bfloat16", "int32", "uint16"
 SCRATCH = {}
-for _d, _l in ((I32, "x0 128 limi 2 ip 32 ipm 32 isl 10 ism 10 f1 6 f1m 6 f2 6 fv 6 fw 6 fa 6 fb 6 fi 6 fks 256 k1 256 k2 256 "
-                     "k3 256 bb 256 di 256 db 256 t1 128 t2 64 v 512 c8 32 mei 32 met 256"),
-               (BF, "mk 128 ml 128 ones 128 idb 128 tri 128 bi 8 pw0 16 pm 16 pw 16 ow 16 bf 256 pbt 256 sw 2048 ge 4096 pre 32"),
-               (F32, "limf 2 orow 128 ie 16 ec 16 ct 32 on32 32 sl9 10 sl8 8 nm 32 zz 32 aa 32 mef 32 idf 128 wk 2048 "
-                     "zo 240 mey 96 od 672 ld 768 a1 192 a2 96 a4 96 a3 96 b1 96 b2 96 yt 97"),
-               (U16, "fp 6 lk 256 pos 32 ks 48 lt 42 lo 6")):
+for _d, _l in ((I32, "x0 128 limi 2 iei 16 iem 16 ip 16 ipm 16 isl 10 ism 10 f1 6 f1m 6 f2 6 fv 6 fw 6 fa 6 fb 6 fi 6 fks 256 "
+                     "k1 256 di 256 db 256 mei 32 cgi 2 kx 48 ky 48"),
+               (BF, "mk 128 ml 128 ones 128 idb 128 prm 128 tri 128 bi0 8 bi 8 pw0 16 pm 16 pw 16 mw 144 bf 256 pbt 256 sw 1024 "
+                    "ge 4096 pre 32 orr 256 rs 128"),
+               (F32, "limf 2 orow 128 ie 16 ct 16 cg 2 sl9 10 sl8 8 zz 32 aa 32 mef 32 met 256 idf 128 wk 2048 kp 256 v 512 "
+                     "zo 240 mey 96 od 768 ld 768 acc 480 b1 96 yt 97"),
+               (U16, "fp 6 lk 256 pos 32 ks 48 lt 48")):
     _w = _l.split()
     for _k in range(0, len(_w), 2):
         SCRATCH[_w[_k]] = ("sbuf", [128, int(_w[_k + 1])], _d)
-SCRATCH["tw"] = ("sbuf", [128, Z0 + R], I32)
-SCRATCH["ds"] = ("dram", [NQ * NH, 128, QP // 8], I32)
-SCRATCH["hs"] = ("dram", [NQ, 128, QP // 8], I32)
-SCRATCH["ds0"] = ("dram", [128, W0 // 8], I32)
-SCRATCH["hs0"] = ("dram", [128, W0 // 8], I32)
-SCRATCH["dl"] = ("dram", [8, 128, 16], BF)
-for _k in ("psa", "psd0", "psd1", "psm"):
+SCRATCH["tw"] = ("sbuf", [128, R + 8], I32)
+SCRATCH["hs"] = ("dram", [240, W0], I32)
+for _k, _l in enumerate(WP):
+    for _w in _l:
+        SCRATCH["hp%d_%d" % (_k, _w)] = ("dram", [240, _w], I32)
+for _k in ("psa", "psd0", "psd1", "psm", "psb"):
     SCRATCH[_k] = ("psum", [128, 512], F32)
-SCRATCH["pst"] = ("psum", [128, 1024], BF)
-SEMAPHORES = (["s%d" % k for k in range(125)] + ["hin%d" % k for k in range(NQ)]
-              + ["mi", "h1", "lx", "lw", "h2", "dx", "dw", "h3", "hsm", "hw", "h0", "h00"])
+for _k in ("w0", "w1", "w2"):
+    SCRATCH[_k] = ("psum", [128, 1024], BF)
+SEMAPHORES = (["s%d" % k for k in range(125)] + ["hin%d" % k for k in range(len(WP))]
+              + ["mi", "h1", "l0", "l1", "l2", "h2", "d0", "d1", "d2", "d3", "d4", "h3", "hsm", "hw", "h0", "h00", "go1", "go2"])
 
 
 def helpers(core, topo):
@@ -46,23 +49,41 @@ def off_chip(core, T, topo):
     return [e for e in es[0] if all(e in x for x in es)]
 
 
+def bits(es):
+    return sum(1 << e for e in es)
+
+
+def feed_engines(owner, T, topo):
+    low = off_chip(owner, T, topo)
+    high = [e for e in topo.engines(owner, helpers(owner, topo)[0]) if e not in low]
+    return [low, high[:len(high) // 2], high[len(high) // 2:]]
+
+
 def hand_on(g, core, T, topo, owner):
-    S, Y, A = T.sem, g.sync, g.scalar
+    S, Y = T.sem, g.sync
     h = helpers(owner, topo).index(core)
-    c0 = Z0 + OWN + W0 + WH * h
-    parts = [(c0 + QP * p, QP, T.hs[p], S["hin%d" % p], 2) for p in range(NQ)]
+    n = len(feed_engines(owner, T, topo)[h])
+    parts = [(C0[k] + sum(w[:h]), w[h], T["hp%d_%d" % (k, w[h])], S["hin%d" % k], n, ((0, 1, 2, 3), (4, 5), (6,)))
+             for k, w in enumerate(WP)]
     if h == 0:
-        parts = [(Z0 + OWN, W0, T.hs0[:], S.hsm, len(off_chip(owner, T, topo)))] + parts
-    for p, (c, w, src, sem, n) in enumerate(parts):
-        for q in (Y, A):
-            q.wait_ge(sem, n)
-        for u in range(8):
-            (Y, A)[u % 2].dma_start(T.tw[16 * u:16 * u + 16, c:c + w], src).then_inc(S["s%d" % p], 16)
+        parts = [(0, W0, T.hs, S.hsm, n, (range(7),))] + parts
+    for p, (c, w, buf, sem, n, calls) in enumerate(parts):
+        Y.wait_ge(sem, n)
+        Y.dma_start(buf[128:240, :], buf[0:112, :]).then_inc(S["s%d" % p], 16)
     rid, pid = topo.addr(owner, core)
-    for p, (c, w, src, sem, n) in enumerate(parts):
-        g.wait_ge(S["s%d" % p], 128)
-        g.remote_dma(T.tw[:, c:c + w], T.tw[:, c:c + w], S.hw, S.h0, pid, rid, topo.mask(core, owner))
-    g.wait_ge(S.h0, len(parts) * len(topo.engines(core, owner)))
+    es = topo.engines(core, owner)
+    sent = 0
+    for p, (c, w, buf, sem, n, calls) in enumerate(parts):
+        g.wait_ge(sem, n)
+        g.wait_ge(S["s%d" % p], 16)
+        for ts in calls:
+            k = len(es) // (len(ts) + len(ts) % 2 if len(ts) > 4 else len(ts))
+            g.remote_dma_fused([RemoteDMATransfer(
+                dst_ids=[DstId(rid=rid, pnc=pid)], dma_engine_mask=bits(es[k * i:k * i + k]), remote_sem=S.hw,
+                srcs=[buf[16 * t + 16:16 * t + 144, :]], dsts=[T.tw[:, BLK * t + c:BLK * t + c + w]])
+                for i, t in enumerate(ts)], local_sem=S.h0)
+            sent += k * len(ts)
+    g.wait_ge(S.h0, sent)
 
 
 def rank_program(g, core, T, topo):
@@ -94,13 +115,10 @@ def rank_program(g, core, T, topo):
         return (name, total[name])
 
     CORES = list(T.cores)
-    half = me // 4
-    other = [r for r in range(8) if r // 4 != half]
-    mine = [r for r in range(8) if r // 4 == half and r != me]
-    peers = other + mine
+    peers = [me ^ x for x in range(1, 8)]
 
-    def slot(src, dst):
-        return src % 4 if src // 4 != dst // 4 else 4 + [r for r in range(8) if r // 4 == dst // 4 and r != dst].index(src)
+    def lcol(x):
+        return 0 if x == 1 else 6 * x - 4 if x < 4 else 6 * x
 
     def at_core(c):
         rid, pid = topo.addr(c, core)
@@ -110,150 +128,170 @@ def rank_program(g, core, T, topo):
         return at_core(CORES[r])
     eng = off_chip(core, T, topo)
     ln2 = math.log(2.0)
-
     hp = helpers(core, topo)
+    fe = feed_engines(core, T, topo)
+
+    def load(a, b):
+        return do("y", [], [lambda u=u: Y.dma_start(T.tw[16 * u:16 * u + 16, S7 + a:S7 + b], T.at[:, BLK * u + a:BLK * u + b])
+                            for u in range(8)], 16)
+
+    def feed(k):
+        for w in sorted(set(WP[k])):
+            g.remote_dma_fused([RemoteDMATransfer(
+                dst_ids=[at_core(c)], dma_engine_mask=bits(fe[i]), remote_sem=S["hin%d" % k],
+                srcs=[T.tw[:, S7 + C0[k] + sum(WP[k][:i]):S7 + C0[k] + sum(WP[k][:i]) + w]], dsts=[T["hp%d_%d" % (k, w)][0:128, :]])
+                for i, c in enumerate(hp) if WP[k][i] == w], local_sem=S.h0)
+        g.sem_inc(S["go%d" % (k + 1)], 1)
+
     t_lim = do("s", [], lambda: A.dma_start(T.limi[0:1, :], T.lim[:]), 16)
     t_x0 = do("y", [], lambda: Y.dma_start(T.x0[:], T.at[0:1, :]), 16)
-    t_ds0 = do("y", [], lambda: Y.dma_start(T.ds0[:], T.at[:, OWN:OWN + W0]), 16)
+    t_ld = [load(0, W0)]
     t_fk = do("s", [], lambda: A.dma_start(T.fks[:], T.fk[:]), 16)
     t_mei = do("s", [], lambda: A.dma_start(T.mei[:], T.me[:]), 16)
-    s0 = OWN + W0
+    t_ld += [load(C0[0], C0[1]), load(C0[1], C0[2])]
 
-    def strip(p):
-        return do("y", [], [lambda h=h, k=k: Y.dma_start(
-            T.ds[NQ * h + k], T.at[:, s0 + WH * h + QP * k:s0 + WH * h + QP * k + QP]) for k in (2 * p, 2 * p + 1) for h in range(NH)], 16)
-    t_ds = [strip(0)]
-    t_vf = do("y", [], lambda: Y.dma_start(T.v[:], T.at[0:4, :]), 16)
-    t_ds.append(strip(1))
-
-    t_ie = do("g", [], lambda: g.iota(T.ie[:], [[-8, 16]], 0, 1, allow_small_or_imprecise_dtypes=True))
-    t_is = do("g", [], lambda: g.iota(T.isl[:], [[-1, 10]], 128, 1))
-    t_ip = do("g", [], lambda: g.iota(T.ip[:], [[1, 32]], 0, 32))
-    t_c8 = do("v", [], [lambda: V.memset(T.c8[:], Z0), lambda: V.memset(T.tw[:, 0:Z0], 0)])
-    t_or = do("v", [], lambda: V.memset(T.orow[0:1, :], 1.0))
+    pat = [[-1, 8], [-64, 2]]
+    t_ie = do("g", [], lambda: g.iota(T.ie[:], pat, 0, 1, allow_small_or_imprecise_dtypes=True))
+    t_iei = do("g", [], lambda: g.iota(T.iei[:], pat, 0, 1))
     t_ones = do("v", [], lambda: V.memset(T.ones[:], 1.0))
-    t_pw0 = do("s", [t_ie], lambda: A.activation(T.pw0[:], T.ie[:], ACT.Exp, bias=7 * ln2, scale=-ln2))
-    t_ec = do("v", [t_ie], lambda: V.tensor_scalar(T.ec[:], T.ie[:], 7.0, 0.0, ALU.min, ALU.max))
+    t_or = do("v", [], lambda: V.memset(T.orow[0:1, :], 1.0))
+    t_z = do("v", [], [lambda: V.memset(T.tw[:, R:R + 8], 0), lambda: V.memset(T.mw[:, 128:144], 0.0)])
+    t_pw0 = do("s", [t_ie], lambda: A.activation(T.pw0[:], T.ie[:], ACT.Exp, bias=7 * ln2, scale=-ln2 / 8))
     t_id = do("g", [t_ones], lambda: g.affine_select(T.idb[:], T.ones[:], [[1, 128]], ALU.is_equal, 0.0, 0, -1))
-    t_sw = [do("v", [], lambda: V.memset(T.sw[:, 0:1024], 0.0))]
-    t_pm = do("v", [t_ec], lambda: V.tensor_tensor(T.pm[:], T.ie[:], T.ec[:], ALU.is_equal))
-    t_ism = do("v", [t_is], lambda: V.tensor_scalar(T.ism[:], T.isl[:], 15, None, ALU.bitwise_and))
-    t_ipm = do("v", [t_ip], lambda: V.tensor_scalar(T.ipm[:], T.ip[:], 511, None, ALU.bitwise_and))
-    t_sl9 = do("v", [t_ism], lambda: V.tensor_scalar(T.sl9[:], T.ism[:], 0.0, None, ALU.is_equal))
-    t_ct = do("v", [t_ipm], lambda: V.tensor_scalar(T.ct[:], T.ipm[:], 769.0, None, ALU.add))
+    t_is = do("g", [], lambda: g.iota(T.isl[:], [[-1, 10]], 128, 1))
+    t_ip = do("g", [], lambda: g.iota(T.ip[:], [[1, 16]], 0, 16))
+    t_vf = [do("v", [], lambda: V.memset(T.v[:, 0:320], float(R)))]
+    t_iem = do("v", [t_iei], lambda: V.tensor_scalar(T.iem[:], T.iei[:], 0xFFC7, None, ALU.bitwise_and))
+    t_pm = do("v", [t_iem], lambda: V.tensor_scalar(T.pm[:], T.iem[:], 0.0, None, ALU.is_equal))
 
-    wait("g", t_ds0)
+    wait("g", t_ld[0])
     rid, pid = topo.addr(hp[0], core)
-    g.remote_dma(T.hs0[:], T.ds0[:], S.hsm, S.h00, pid, rid, sum(1 << e for e in eng))
+    g.remote_dma(T.hs[0:128, :], T.tw[:, S7:S7 + W0], S.hsm, S.h00, pid, rid, bits(eng))
 
     t_lf = do("v", [t_lim], lambda: V.tensor_copy(T.limf[0:1, :], T.limi[0:1, :]))
     t_pl = do("t", [t_or, t_lf], lambda: P.matmul(T.psa[:, 0:2], T.orow[0:1, :], T.limf[0:1, :], True, True))
-    t_sw.append(do("v", [], lambda: V.memset(T.sw[:, 1024:1536], 0.0)))
+    t_vf.append(do("v", [], lambda: V.memset(T.v[:, 320:512], float(R))))
     t_ml = do("v", [t_x0, t_pl], [lambda: V.tensor_scalar(T.ml[:], T.x0[:], T.psa[:, 0:1], None, ALU.is_lt),
                                   lambda: V.tensor_scalar(T.mk[:], T.x0[:], T.psa[:, 1:2], None, ALU.is_gt)])
     t_pw = do("v", [t_pw0, t_pm], lambda: V.tensor_tensor(T.pw[:], T.pw0[:], T.pm[:], ALU.mult))
     t_pp = do("t", [t_ml, t_pw], [lambda: P.matmul(T.psa[:, 16:32], T.ml[:], T.pw[:], True, False),
                                   lambda: P.matmul(T.psa[:, 16:32], T.mk[:], T.pw[:], False, True)])
-    t_k1 = do("v", [t_fk], lambda: V.tensor_scalar(T.k1[:], T.fks[:], 0x3C7F, None, ALU.bitwise_and))
-    t_own = do("v", [t_pp], lambda: V.tensor_copy(T.ow[:], T.psa[:, 16:32]))
-    wait("g", t_own)
-    g.remote_dma_fused([RemoteDMATransfer(dst_ids=[dest(r) for r in peers], dma_engine_mask=sum(1 << e for e in eng),
-                                          remote_sem=S.mi, srcs=[T.ow[:]], dsts=[T.dl[me] for r in peers])], local_sem=S.h1)
-
-    he = topo.engines(core, hp[0])[::-1]
-
-    def strips(p):
-        todo = [(i, c, k) for k in (2 * p, 2 * p + 1) for i, c in enumerate(hp)]
-        g.remote_dma_fused([RemoteDMATransfer(dst_ids=[at_core(c)], dma_engine_mask=(1 << he[2 * j]) | (1 << he[2 * j + 1]),
-                                              remote_sem=S["hin%d" % k], srcs=[T.ds[NQ * i + k]], dsts=[T.hs[k]])
-                            for j, (i, c, k) in enumerate(todo)], local_sem=S.h0)
-    wait("g", t_ds[0])
-    strips(0)
-
-    t_k2 = do("v", [t_k1], lambda: V.tensor_scalar(T.k2[:], T.k1[:], 16.0 + 1.0 / 1024.0, None, ALU.mult))
-    t_bb = do("v", [t_fk], lambda: V.tensor_scalar(T.bb[:], T.fks[:], 7, 7, ALU.arith_shift_right, ALU.bitwise_and))
-    t_sw.append(do("v", [], lambda: V.memset(T.sw[:, 1536:2048], 0.0)))
-    t_k3 = do("v", [t_k2], lambda: V.tensor_scalar(T.k3[:], T.k2[:], 2047, None, ALU.bitwise_and))
-    t_bf = do("v", [t_bb], [lambda c=c: V.tensor_copy(T.bf[:, 128 * c:128 * c + 128], T.bb[:, c::2]) for c in range(2)])
-    t_lk = do("v", [t_k3], [lambda c=c: V.tensor_copy(T.lk[:, 128 * c:128 * c + 128], T.k3[:, c::2]) for c in range(2)])
     t_mef = do("v", [t_mei], lambda: V.tensor_copy(T.mef[:], T.mei[:]))
+    ow = T.mw[:, 16 * me:16 * me + 16]
+    t_own = do("v", [t_pp], lambda: V.tensor_copy(ow, T.psa[:, 16:32]))
+    wait("g", t_own)
+    g.remote_dma_fused([RemoteDMATransfer(dst_ids=[dest(r) for r in peers], dma_engine_mask=bits(eng),
+                                          remote_sem=S.mi, srcs=[ow], dsts=[ow for r in peers])], local_sem=S.h1)
+    for k in range(2):
+        wait("g", t_ld[k + 1])
+        feed(k)
+    wait("y", ("go1", 1))
+    t_ld.append(load(C0[2], BLK))
 
-    t_on32 = do("s", [t_ones], lambda: A.activation(T.on32[:], T.ones[:, 0:32], ACT.Copy))
-    t_sl8 = do("s", [t_sl9], lambda: A.activation(T.sl8[:], T.sl9[:, 0:8], ACT.Identity, bias=T.sl9[:, 8:9]))
-    t_idf = do("s", [t_id], lambda: A.activation(T.idf[:], T.idb[:], ACT.Copy))
-    t_wkz = do("s", [t_sw[0]], lambda: A.activation(T.wk[:, 0:768], T.sw[:, 0:768], ACT.Copy, scale=0.0))
-    t_bt = do("t", [t_id, t_bf], [lambda c=c: P.transpose(
-        T.pst[:, 128 * c:128 * c + 128], T.bf[:, 128 * c:128 * c + 128], T.idb[:]) for c in range(2)])
-    t_pbt = do("s", [t_bt], lambda: A.activation(T.pbt[:], T.pst[:, 0:256], ACT.Exp, scale=ln2))
-    t_mt = do("t", [t_mef, t_idf], [lambda c=c: P.matmul(
-        T.psm[0:16, c:256:2], T.mef[:, 16 * c:16 * c + 16], T.idf[:], True, True) for c in range(2)])
+    t_bf = do("v", [t_fk], lambda: V.tensor_scalar(T.bf[:], T.fks[:], 1.0 / 1024, 191.5 + 1.0 / 2048, ALU.mult, ALU.add))
+    t_k1 = do("v", [], lambda: V.tensor_scalar(T.k1[:], T.fks[:], 1023, None, ALU.bitwise_and))
+    t_kp = do("v", [], [lambda c=c: V.tensor_copy(T.kp[:, c::2], T.fks[:, 128 * c:128 * c + 128]) for c in range(2)])
+    t_lk = do("v", [t_k1], lambda: V.tensor_copy(T.lk[:], T.k1[:]))
+    t_ism = do("v", [t_is], lambda: V.tensor_scalar(T.ism[:], T.isl[:], 15, None, ALU.bitwise_and))
+    t_ipm = do("v", [t_ip], [lambda: V.tensor_scalar(T.ipm[:], T.ip[:], 255, None, ALU.bitwise_and),
+                             lambda: V.tensor_scalar(T.cgi[:], T.ip[:, 0:2], 8, None, ALU.arith_shift_right)])
+    t_sl9 = do("v", [t_ism], lambda: V.tensor_scalar(T.sl9[:], T.ism[:], 0.0, None, ALU.is_equal))
+    t_ct = do("v", [t_ipm], [lambda: V.tensor_scalar(T.ct[:], T.ipm[:], 769.0, None, ALU.add),
+                             lambda: V.tensor_scalar(T.cg[:], T.cgi[:], -float(BLK), -float(BLK), ALU.mult, ALU.add)])
 
-    t_dl = do("y", [t_own], lambda: Y.dma_start(T.dl[me], T.ow[:]), 16)
-    t_win = do("y", [t_dl, t_wkz, ("mi", 7 * len(eng))] + t_sw, lambda: Y.dma_start(T.sw[0::16, :], T.dl[:]), 16)
-    wait("y", t_vf, t_c8)
-    t_v = do("y", [], [lambda q=q: Y.dma_start(T.v[16 * q:16 * q + 8, :], T.fk[:, 32 * q:32 * q + 32]) for q in range(8)]
-             + [lambda: Y.dma_start(T.v[8::16, :], T.c8[:])], 16)
-
-    t_bi = do("g", [], lambda: g.affine_select(T.bi[:], T.ones[:, 0:8], [[-16, 8]], ALU.is_equal, 0.0, 0, 1))
+    t_pe = do("g", [], lambda: g.affine_select(T.prm[:], T.ones[:], [[-1, 16], [-16, 8]], ALU.is_equal, 0.0, 0, 1))
+    t_bi0 = do("g", [], lambda: g.affine_select(T.bi0[:], T.ones[:, 0:8], [[-16, 8]], ALU.is_equal, 0.0, 0, 1))
     t_tri = do("g", [], lambda: g.affine_select(T.tri[:], T.ones[:], [[1, 128]], ALU.is_gt, 0.0, 0, -1))
+    t_bi = do("g", [t_bi0], lambda: g.affine_select(T.bi[:], T.bi0[:], [[-16, 8]], ALU.not_equal, 1.0 / 256, -1, 1))
     t_f = do("g", [], [lambda: g.iota(T.f1[:], [[0, 6]], 0, 1), lambda: g.iota(T.f2[:], [[16, 6]], 0, 0)])
-    wait("g", t_win, t_ds[1])
-    strips(1)
 
-    sw = T.sw[:, 0:2048]
-    t_gv, t_gs = [], []
-    for c in range(2):
-        o, l = 2048 * c, 128 * c
-        t_gv.append(do("v", [t_win, t_lk], lambda: V.tensor_copy(T.ge[:, o:o + 1024], sw.indirect(T.lk[:, l:l + 64]))))
-        t_gs.append(do("s", [t_win, t_lk], lambda: A.activation(
-            T.ge[:, o + 1024:o + 2048], sw.indirect(T.lk[:, l + 64:l + 128]), ACT.Copy)))
-        if c == 0:
-            t_met = do("v", [t_mt], lambda: V.tensor_copy(T.met[0:16, :], T.psm[0:16, 0:256]))
+    t_idf = do("s", [t_id], lambda: A.activation(T.idf[:], T.idb[:], ACT.Copy))
+    t_wkz = do("s", t_vf, [lambda: A.activation(T.wk[:, 0:512], T.v[:, 0:512], ACT.Copy, scale=0.0),
+                           lambda: A.activation(T.wk[:, 512:776], T.v[:, 0:264], ACT.Copy, scale=0.0)])
+    t_rs0 = do("s", [t_ones], lambda: A.activation(T.rs[:], T.ones[:], ACT.Copy))
+    t_mt = do("t", [t_mef, t_idf], [lambda c=c, h=h: P.matmul(
+        T.psm[0:16, 2 * h + c:256:4], T.mef[:, 16 * h:16 * h + 16], T.idf[:, 64 * c:64 * c + 64], True, True)
+        for c in range(2) for h in range(2)])
+    t_met = do("s", [t_mt], lambda: A.activation(T.met[0:16, :], T.psm[0:16, 0:256], ACT.Copy))
+    t_rs = do("s", [t_rs0], lambda: A.activation(T.rs[:, 0::8], T.ones[:, 0:16], ACT.Copy, scale=0.0))
+    t_bt = do("t", [t_pe, t_bf], [lambda c=c: P.matmul(
+        T.psb[:, 128 * c:128 * c + 128], T.bf[:, 128 * c:128 * c + 128], T.prm[:], True, True) for c in range(2)])
+    t_pbt = do("s", [t_bt], lambda: A.activation(T.pbt[:], T.psb[:, 0:256], ACT.Exp, bias=(8 - 192) * ln2, scale=ln2))
+    t_sl8 = do("s", [t_sl9], lambda: A.activation(T.sl8[:], T.sl9[:, 0:8], ACT.Identity, bias=T.sl9[:, 8:9]))
+
+    t_mr = do("y", [t_met, t_wkz] + t_vf, [lambda q=q: Y.dma_start(
+        T.v[16 * q + 9:16 * q + 10, :], T.met[0:16, 32 * q:32 * q + 32]) for q in range(8)], 16)
+    t_v = do("y", [t_kp, ("go2", 1)], [lambda q=q: Y.dma_start(
+        T.v[16 * q:16 * q + 8, :], T.kp[:, 32 * q:32 * q + 32]) for q in range(8)], 16)
+    wait("y", t_ld[3])
+    a, b = C0[-1], BLK
+    t_tw = do("y", [], [lambda t=t, lo=lo, hi=hi, src=src: Y.dma_start(
+        T.tw[lo:hi, BLK * t + a:BLK * t + b], T.tw[src:src + hi - lo, S7 + a:S7 + b])
+        for t in range(7) for lo, hi, src in ((0, 112 - 16 * t, 16 * t + 16), (112 - 16 * t, 128, 0))], 16)
+
+    wait("t", ("mi", 7 * len(eng)), t_own, t_z, t_id)
+    t_win = []
+    for ps, ts, q in ((T.w0, (0, 1, 2), "s"), (T.w1, (3, 4, 5), "v"), (T.w2, (6, 7), "v")):
+        t_t = do("t", [], [lambda i=i, t=t: P.transpose(ps[:, 128 * i:128 * i + 128], T.mw[:, 2 * t:2 * t + 128], T.idb[:])
+                           for i, t in enumerate(ts)])
+        o, n = 128 * ts[0], 128 * len(ts)
+        t_win.append(do(q, [t_t], (lambda: A.activation(T.sw[:, o:o + n], ps[:, 0:n], ACT.Copy)) if q == "s"
+                        else (lambda: V.tensor_copy(T.sw[:, o:o + n], ps[:, 0:n]))))
+
+    sw = T.sw[:, 0:1024]
+    wait("v", t_lk, *t_win)
+    wait("s", t_lk, *t_win)
+    t_gv = [do("v", [], lambda: V.tensor_copy(T.ge[:, 16 * a:16 * b], sw.indirect(T.lk[:, a:b]))) for a, b in ((0, 64), (128, 128 + VG))]
+    t_gs = [do("s", [], lambda: A.activation(T.ge[:, 16 * a:16 * b], sw.indirect(T.lk[:, a:b]), ACT.Copy))
+            for a, b in ((64, 128), (128 + VG, 256))]
     t_zoz = do("s", [t_gs[0]], lambda: A.activation(T.zo[:], T.ge[:, 1024:1264], ACT.Copy, scale=0.0))
     t_zo = do("s", [t_zoz, t_sl9], lambda: A.activation(T.zo[:, 112:128], T.zo[:, 0:16], ACT.Identity, bias=T.sl9[:, 9:10]))
-    t_tw = [do("y", [], lambda: Y.dma_start(T.tw[0:16, Z0:Z0 + OWN], T.at[:, 0:OWN]), 16)]
-    t_mr = do("y", [t_met], [lambda q=q: Y.dma_start(T.v[16 * q + 9:16 * q + 10, :], T.met[0:16, 32 * q:32 * q + 32]) for q in range(8)], 16)
-    t_tw.append(do("y", [], [lambda u=u: Y.dma_start(
-        T.tw[16 * u:16 * u + 16, Z0:Z0 + OWN], T.at[:, 0:OWN]) for u in range(1, 8)], 16))
 
-    t_m = []
+    t_wk, t_pos, t_dis, t_pres = t_wkz, t_own, [], []
     for c in range(2):
         ps = (T.psd0, T.psd1)[c]
-        o, a, b, e = 128 * c, 64 * c, 32 * c, 16 * c
+        o, a, e = 128 * c, 64 * c, 16 * c
+        tot = T.pre[:, e + 15:e + 16]
         t_d = do("t", [t_bi, t_gv[c], t_gs[c]], [lambda q=q: P.matmul(
-            ps[:, q:128:16], T.ge[:, 2048 * c + q:2048 * c + 2048:16], T.bi[:], True, True) for q in range(16)])
+            ps[:, 8 * q:8 * q + 8], T.ge[:, 2048 * c + q:2048 * c + 2048:16], T.bi[:], True, True) for q in range(16)])
         t_di = do("v", [t_d, t_pbt], lambda: V.tensor_tensor(T.di[:, o:o + 128], ps[:, 0:128], T.pbt[:, o:o + 128], ALU.mult))
         t_db = do("v", [t_di], lambda: V.tensor_scalar(
-            T.db[:, o:o + 128], T.di[:, o:o + 128], 7, 1, ALU.logical_shift_right, ALU.bitwise_and))
-        t_1 = do("v", [t_db], lambda: V.tensor_tensor(T.t1[:, a:a + 64], T.db[:, o:o + 64], T.db[:, o + 64:o + 128], ALU.max))
-        t_2 = do("v", [t_1], lambda: V.tensor_tensor(T.t2[:, b:b + 32], T.t1[:, a:a + 32], T.t1[:, a + 32:a + 64], ALU.max))
-        t_m.append(do("v", [t_2], lambda: V.tensor_tensor(T.nm[:, e:e + 16], T.t2[:, b:b + 16], T.t2[:, b + 16:b + 32], ALU.max)))
+            T.db[:, o:o + 128], T.di[:, o:o + 128], 15, 1, ALU.logical_shift_right, ALU.bitwise_and))
+        t_o = do("v", [t_db, t_rs], lambda: V.tensor_tensor_scan(T.orr[:, o:o + 128], T.rs[:], T.db[:, o:o + 128], 0.0, ALU.mult, ALU.max))
+        nm = T.orr[:, o + 7:o + 128:8]
+        t_pre = do("v", [t_o, t_ones], lambda: V.tensor_tensor_scan(T.pre[:, e:e + 16], T.ones[:, 0:16], nm, 0.0, ALU.add, ALU.subtract))
+        mms = [lambda: P.matmul(T.psa[:, 64 + c:65 + c], T.tri[:], tot, True, True)]
+        if c == 0:
+            mms.append(lambda: P.matmul(T.psa[:, 66:67], T.ones[:], tot, True, True))
+        t_off = do("t", [t_tri, t_pos, t_pre], mms)
+        t_zz = do("v", [t_ct], lambda: V.tensor_tensor(T.zz[:, e:e + 16], nm, T.ct[:], ALU.mult))
+        t_aa = do("v", [t_zz, t_pre], lambda: V.tensor_tensor(T.aa[:, e:e + 16], T.pre[:, e:e + 16], T.zz[:, e:e + 16], ALU.add))
+        t_pos = do("v", [t_aa, t_off], lambda: V.tensor_scalar(
+            T.pos[:, e:e + 16], T.aa[:, e:e + 16], T.psa[:, 64 + c:65 + c], T.psa[:, 66:67] if c else 0.0, ALU.add, ALU.add))
+        t_wk = do("v", [t_pos, t_wk, t_v, t_mr] + t_vf, lambda: V.tensor_copy(
+            T.wk[:, 0:2048].indirect(T.pos[:, e:e + 16]), T.v[:, c::2]))
+        t_dis.append(t_di)
+        t_pres.append(t_pre)
+    t_nn = do("t", [t_met] + t_pres, [lambda c=c: P.matmul(T.psm[:, 256:257], T.ones[:], T.pre[:, 16 * c + 15:16 * c + 16], c == 0, c == 1)
+                                      for c in range(2)])
+    t_n = do("v", [t_nn], lambda: V.tensor_copy(T.yt[:, 96:97], T.psm[:, 256:257]))
 
-    t_pre = do("v", [t_on32] + t_m, lambda: V.tensor_tensor_scan(T.pre[:], T.on32[:], T.nm[:], 0.0, ALU.add, ALU.subtract))
-    t_off = do("t", [t_tri, t_ones, t_own, t_pre], [
-        lambda: P.matmul(T.psa[:, 64:65], T.tri[:], T.pre[:, 31:32], True, True),
-        lambda: P.matmul(T.psa[:, 65:66], T.ones[:], T.pre[:, 31:32], True, True)])
-    t_zz = do("v", [t_ct], lambda: V.tensor_tensor(T.zz[:], T.nm[:], T.ct[:], ALU.mult))
-    t_aa = do("v", [t_zz, t_pre], lambda: V.tensor_tensor(T.aa[:], T.pre[:], T.zz[:], ALU.add))
-    t_pos = do("v", [t_aa, t_off], lambda: V.tensor_scalar(T.pos[:], T.aa[:], T.psa[:, 64:65], -1.0, ALU.add, ALU.add))
-
-    wait("v", t_v, t_mr, t_vf)
-    t_wk = t_wkz
-    for c in range(2):
-        t_wk = do("v", [t_pos, t_wk], lambda: V.tensor_copy(T.wk[:, 0:2048].indirect(T.pos[:, 16 * c:16 * c + 16]), T.v[:, c::2]))
-    t_n = do("v", [], lambda: V.tensor_copy(T.yt[:, 96:97], T.psa[:, 65:66]))
-    t_k = do("t", [t_wk, t_sl8, t_pos, t_n], [lambda c=c: P.matmul(
-        T.psa[:, 128 + c:176:6], T.wk[:, c:768:6], T.sl8[:], True, True) for c in range(6)])
-    t_ks = do("v", [t_k], lambda: V.tensor_copy(T.ks[:], T.psa[:, 128:176]))
-    t_lo = do("v", [], lambda: V.tensor_copy(T.lo[:], T.psa[:, 128 + 6 * me:134 + 6 * me]))
+    t_k = do("t", [t_wk, t_sl8, t_dis[0]], [lambda c=c: P.matmul(
+        T.psd0[:, c:48:6], T.wk[:, 1 + c:769:6], T.sl8[:], True, True) for c in range(6)])
+    t_kx = do("v", [t_k], lambda: V.tensor_scalar(T.kx[:], T.psd0[:, 0:48], T.cg[:, 0:1], None, ALU.add))
+    t_ky = do("v", [t_kx], lambda: V.tensor_scalar(T.ky[:], T.kx[:], 0x10000 + R - 1, None, ALU.bitwise_and))
+    t_ks = do("v", [t_ky], lambda: V.tensor_scalar(T.ks[:], T.ky[:], float(R), None, ALU.min))
 
     wait("g", t_ks)
-    g.remote_dma_fused([RemoteDMATransfer(
-        dst_ids=[dest(r)], dma_engine_mask=1 << eng[i], remote_sem=S.lx if r in other else S.lw,
-        srcs=[T.ks[:, 6 * r:6 * r + 6]], dsts=[T.lt[:, 6 * slot(me, r):6 * slot(me, r) + 6]]) for i, r in enumerate(peers)], local_sem=S.h2)
+    for k, xs in enumerate(HOP2):
+        n = len(eng) // len(xs)
+        g.remote_dma_fused([RemoteDMATransfer(
+            dst_ids=[dest(me ^ x)], dma_engine_mask=bits(eng[n * i:n * i + n]), remote_sem=S["l%d" % k],
+            srcs=[T.ks[:, 6 * (me ^ x):6 * (me ^ x) + 6]], dsts=[T.lt[:, lcol(x):lcol(x) + 6]])
+            for i, x in enumerate(xs)], local_sem=S.h2)
 
-    t_me = do("t", [t_wk, t_zo, t_met], [lambda u=u: P.matmul(
-        T.psm[:, 0:96], T.zo[:, 112 - 16 * u:240 - 16 * u], T.wk[:, 96 * u:96 * u + 96], u == 0, u == 7) for u in range(8)])
+    t_me = do("t", [t_wk, t_zo, t_n], [lambda u=u: P.matmul(
+        T.psm[:, 0:96], T.zo[:, 112 - 16 * u:240 - 16 * u], T.wk[:, 1 + 96 * u:97 + 96 * u], u == 0, u == 7) for u in range(8)])
     t_mey = do("s", [t_me], lambda: A.activation(T.mey[:], T.psm[:, 0:96], ACT.Copy))
 
     t_f1m = do("v", [t_f], lambda: V.tensor_scalar(T.f1m[:], T.f1[:], 15, None, ALU.bitwise_and))
@@ -264,34 +302,36 @@ def rank_program(g, core, T, topo):
     t_fi = do("v", [t_fa], lambda: V.tensor_tensor(T.fi[:], T.fa[:], T.fb[:], ALU.add))
     t_fp = do("v", [t_fi], lambda: V.tensor_copy(T.fp[:], T.fi[:]))
 
-    win = T.tw[:, 0:Z0 + R]
-    nw = sum((NQ + 1 if i == 0 else NQ) * len(topo.engines(c, core)) for i, c in enumerate(hp))
-    wait("v", *t_tw, t_c8, ("hw", nw), ("lx", 4))
-    t_ox = do("v", [], lambda: V.tensor_copy(T.od[:, 0:384], win.indirect(T.lt[:, 0:24])))
-    wait("v", ("lw", 3))
-    t_ow = do("v", [], lambda: V.tensor_copy(T.od[:, 384:672], win.indirect(T.lt[:, 24:42])))
-    t_oo = do("v", [t_lo], lambda: V.tensor_copy(T.ld[:, 672:768], win.indirect(T.lo[:, 0:6])))
-    for tok, rs, sem in ((t_ox, other, "dx"), (t_ow, mine, "dw")):
-        wait("g", tok)
+    win = T.tw[:, 0:R + 8]
+    ne = len(topo.engines(hp[0], core))
+    wait("v", t_tw, t_z, *t_ld)
+    wait("v", ("hw", 7 * (ne // 8) + NH * len(WP) * 3 * ne))
+    for k, xs in enumerate(HOP3):
+        x, n = xs[0], len(eng) // len(xs)
+        landed = ("l%d" % [j for j, ys in enumerate(HOP2) if x in ys][0], len(eng))
+        wait("g", do("v", [landed], lambda: V.tensor_copy(
+            T.od[:, 96 * x:96 * (x + len(xs))], win.indirect(T.lt[:, lcol(x):lcol(x) + 6 * len(xs)]))))
         g.remote_dma_fused([RemoteDMATransfer(
-            dst_ids=[dest(r)], dma_engine_mask=(1 << eng[2 * i]) | (1 << eng[2 * i + 1]), remote_sem=S[sem],
-            srcs=[T.od[:, 96 * slot(r, me):96 * slot(r, me) + 96]],
-            dsts=[T.ld[:, 96 * slot(me, r):96 * slot(me, r) + 96]]) for i, r in enumerate(rs)], local_sem=S.h3)
+            dst_ids=[dest(me ^ x)], dma_engine_mask=bits(eng[n * i:n * i + n]), remote_sem=S["d%d" % k],
+            srcs=[T.od[:, 96 * x:96 * x + 96]], dsts=[T.ld[:, 96 * x:96 * x + 96]]) for i, x in enumerate(xs)], local_sem=S.h3)
+    t_oo = do("v", [t_ks], lambda: V.tensor_copy(T.ld[:, 0:96], win.indirect(T.ks[:, 6 * me:6 * me + 6])))
 
-    wait("v", ("dx", 8))
-    t_a1 = do("v", [], lambda: V.tensor_tensor(T.a1[:], T.ld[:, 0:192], T.ld[:, 192:384], ALU.add))
-    t_a2 = do("v", [t_a1], lambda: V.tensor_tensor(T.a2[:], T.a1[:, 0:96], T.a1[:, 96:192], ALU.add))
-    t_a4 = do("v", [t_a2, t_oo], lambda: V.tensor_tensor(T.a4[:], T.a2[:], T.ld[:, 672:768], ALU.add))
-    t_a3 = do("v", [t_a4, t_fp, t_mey], lambda: V.tensor_tensor(T.a3[:], T.a4[:, 0:96].indirect(T.fp[:, 0:6]), T.mey[:], ALU.add))
-    wait("v", ("dw", 6))
-    t_b1 = do("v", [], lambda: V.tensor_tensor(T.b1[:], T.ld[:, 384:480], T.ld[:, 480:576], ALU.add))
-    t_b2 = do("v", [t_a3], lambda: V.tensor_tensor(T.b2[:], T.ld[:, 576:672].indirect(T.fp[:, 0:6]), T.a3[:], ALU.add))
-    t_y = do("v", [t_b1, t_b2], lambda: V.tensor_tensor(T.yt[:, 0:96], T.b1[:, 0:96].indirect(T.fp[:, 0:6]), T.b2[:], ALU.add))
+    fp = T.fp[:, 0:6]
+    t_y = do("v", [t_oo, t_fp, t_mey], lambda: V.tensor_tensor(T.acc[:, 0:96], T.ld[:, 0:96].indirect(fp), T.mey[:], ALU.add))
+    for k, xs in enumerate(HOP3):
+        src = T.ld[:, 96 * xs[0]:96 * xs[0] + 96]
+        wait("v", ("d%d" % k, len(eng)))
+        if len(xs) == 2:
+            pair = T.od[:, 0:96] if k % 2 else T.b1[:, 0:96]
+            wait("v", do("v", [], lambda: V.tensor_tensor(pair, src, T.ld[:, 96 * xs[1]:96 * xs[1] + 96], ALU.add)))
+            src = pair
+        out = T.yt[:, 0:96] if k == len(HOP3) - 1 else T.acc[:, 96 * k + 96:96 * k + 192]
+        t_y = do("v", [t_y], lambda: V.tensor_tensor(out, src.indirect(fp), T.acc[:, 96 * k:96 * k + 96], ALU.add))
     done = []
     for q, us in (("y", range(0, 4)), ("s", range(4, 8))):
         done.append(do(q, [t_y, t_n], [lambda u=u: Q[q].dma_start(
             T.y[:, 96 * u:96 * u + (97 if u == 7 else 96)], T.yt[16 * u:16 * u + 16, 0:97 if u == 7 else 96]) for u in us], 16))
     wait("y", *done)
-    wait("g", ("h1", len(eng)), ("h3", 14), ("h2", 7), ("h0", 8 * NH), ("h00", len(eng)))
+    wait("g", ("h1", len(eng)), ("h3", len(HOP3) * len(eng)), ("h2", len(HOP2) * len(eng)), ("h0", len(WP) * sum(len(x) for x in fe)), ("h00", len(eng)))
     waited = {name for _, name in seen}
     wait("g", *[(n, t) for n, t in total.items() if n not in waited])

import math
import numpy as np
from concourse.bass import DstId, RemoteDMATransfer
from concourse.mybir import dt, AluOpType, AxisListType, ActivationFunctionType

ALU = AluOpType
ACT = ActivationFunctionType
R, BLK = 16384, 2048
S7 = 7 * BLK
NH = 3
W0 = 32
HOP2 = ((1,), (2, 3), (4, 5, 6, 7))
HOP3 = ((1,), (2, 3), (4, 5), (6,), (7,))
WP = ((184, 184, 184), (184, 184, 184))
C0 = [W0 + sum(sum(w) for w in WP[:k]) for k in range(len(WP) + 1)]
VG = 24

F32, BF, I32, U16 = "float32", "bfloat16", "int32", "uint16"
SCRATCH = {}
for _d, _l in ((I32, "x0 128 limi 2 iei 16 iem 16 ip 16 ipm 16 isl 10 ism 10 f1 6 f1m 6 f2 6 fv 6 fw 6 fa 6 fb 6 fi 6 fks 256 "
                     "k1 256 di 256 db 256 mei 32 cgi 2 kx 48 ky 48"),
               (BF, "mk 128 ml 128 ones 128 idb 128 prm 128 tri 128 bi0 8 bi 8 pw0 16 pm 16 pw 16 mw 144 bf 256 pbt 256 sw 1024 "
                    "ge 4096 pre 32 orr 256 rs 128"),
               (F32, "limf 2 orow 128 ie 16 ct 16 cg 2 sl9 10 sl8 8 zz 32 aa 32 mef 32 met 256 idf 128 wk 2048 kp 256 v 512 "
                     "zo 240 mey 96 od 768 ld 768 acc 480 b1 96 yt 97"),
               (U16, "fp 6 lk 256 pos 32 ks 48 lt 48")):
    _w = _l.split()
    for _k in range(0, len(_w), 2):
        SCRATCH[_w[_k]] = ("sbuf", [128, int(_w[_k + 1])], _d)
SCRATCH["tw"] = ("sbuf", [128, R + 8], I32)
SCRATCH["hs"] = ("dram", [240, W0], I32)
for _k, _l in enumerate(WP):
    for _w in _l:
        SCRATCH["hp%d_%d" % (_k, _w)] = ("dram", [240, _w], I32)
for _k in ("psa", "psd0", "psd1", "psm", "psb"):
    SCRATCH[_k] = ("psum", [128, 512], F32)
for _k in ("w0", "w1", "w2"):
    SCRATCH[_k] = ("psum", [128, 1024], BF)
SEMAPHORES = (["s%d" % k for k in range(125)] + ["hin%d" % k for k in range(len(WP))]
              + ["mi", "h1", "l0", "l1", "l2", "h2", "d0", "d1", "d2", "d3", "d4", "h3", "hsm", "hw", "h0", "h00", "go1", "go2"])


def helpers(core, topo):
    return [c for c in topo.cores_of(core) if c != core and topo.die(c) == topo.die(core)][:NH]


def off_chip(core, T, topo):
    es = [topo.engines(core, c) for c in T.cores if c != core]
    return [e for e in es[0] if all(e in x for x in es)]


def bits(es):
    return sum(1 << e for e in es)


def feed_engines(owner, T, topo):
    low = off_chip(owner, T, topo)
    high = [e for e in topo.engines(owner, helpers(owner, topo)[0]) if e not in low]
    return [low, high[:len(high) // 2], high[len(high) // 2:]]


def hand_on(g, core, T, topo, owner):
    S, Y = T.sem, g.sync
    h = helpers(owner, topo).index(core)
    n = len(feed_engines(owner, T, topo)[h])
    parts = [(C0[k] + sum(w[:h]), w[h], T["hp%d_%d" % (k, w[h])], S["hin%d" % k], n, ((0, 1, 2, 3), (4, 5), (6,)))
             for k, w in enumerate(WP)]
    if h == 0:
        parts = [(0, W0, T.hs, S.hsm, n, (range(7),))] + parts
    for p, (c, w, buf, sem, n, calls) in enumerate(parts):
        Y.wait_ge(sem, n)
        Y.dma_start(buf[128:240, :], buf[0:112, :]).then_inc(S["s%d" % p], 16)
    rid, pid = topo.addr(owner, core)
    es = topo.engines(core, owner)
    sent = 0
    for p, (c, w, buf, sem, n, calls) in enumerate(parts):
        g.wait_ge(sem, n)
        g.wait_ge(S["s%d" % p], 16)
        for ts in calls:
            k = len(es) // (len(ts) + len(ts) % 2 if len(ts) > 4 else len(ts))
            g.remote_dma_fused([RemoteDMATransfer(
                dst_ids=[DstId(rid=rid, pnc=pid)], dma_engine_mask=bits(es[k * i:k * i + k]), remote_sem=S.hw,
                srcs=[buf[16 * t + 16:16 * t + 144, :]], dsts=[T.tw[:, BLK * t + c:BLK * t + c + w]])
                for i, t in enumerate(ts)], local_sem=S.h0)
            sent += k * len(ts)
    g.wait_ge(S.h0, sent)


def rank_program(g, core, T, topo):
    me = T.rank_of(core)
    if me is None:
        for c in T.cores:
            if core in helpers(c, topo):
                hand_on(g, core, T, topo, c)
        return
    S = T.sem
    Q = {"g": g, "v": g.vector, "s": g.scalar, "y": g.sync, "t": g.tensor}
    V, A, P, Y = g.vector, g.scalar, g.tensor, g.sync
    count, seen, total = [0], {}, {}

    def wait(q, *toks):
        for name, val in toks:
            if seen.get((q, name), 0) < val:
                Q[q].wait_ge(S[name], val)
                seen[(q, name)] = val

    def do(q, deps, fns, n=1):
        wait(q, *deps)
        fns = fns if isinstance(fns, list) else [fns]
        name = "s%d" % count[0]
        count[0] += 1
        for f in fns:
            f().then_inc(S[name], n)
        total[name] = n * len(fns)
        return (name, total[name])

    CORES = list(T.cores)
    peers = [me ^ x for x in range(1, 8)]

    def lcol(x):
        return 0 if x == 1 else 6 * x - 4 if x < 4 else 6 * x

    def at_core(c):
        rid, pid = topo.addr(c, core)
        return DstId(rid=rid, pnc=pid)

    def dest(r):
        return at_core(CORES[r])
    eng = off_chip(core, T, topo)
    ln2 = math.log(2.0)
    hp = helpers(core, topo)
    fe = feed_engines(core, T, topo)

    def load(a, b):
        return do("y", [], [lambda u=u: Y.dma_start(T.tw[16 * u:16 * u + 16, S7 + a:S7 + b], T.at[:, BLK * u + a:BLK * u + b])
                            for u in range(8)], 16)

    def feed(k):
        for w in sorted(set(WP[k])):
            g.remote_dma_fused([RemoteDMATransfer(
                dst_ids=[at_core(c)], dma_engine_mask=bits(fe[i]), remote_sem=S["hin%d" % k],
                srcs=[T.tw[:, S7 + C0[k] + sum(WP[k][:i]):S7 + C0[k] + sum(WP[k][:i]) + w]], dsts=[T["hp%d_%d" % (k, w)][0:128, :]])
                for i, c in enumerate(hp) if WP[k][i] == w], local_sem=S.h0)
        g.sem_inc(S["go%d" % (k + 1)], 1)

    t_lim = do("s", [], lambda: A.dma_start(T.limi[0:1, :], T.lim[:]), 16)
    t_x0 = do("y", [], lambda: Y.dma_start(T.x0[:], T.at[0:1, :]), 16)
    t_ld = [load(0, W0)]
    t_fk = do("s", [], lambda: A.dma_start(T.fks[:], T.fk[:]), 16)
    t_mei = do("s", [], lambda: A.dma_start(T.mei[:], T.me[:]), 16)
    t_ld += [load(C0[0], C0[1]), load(C0[1], C0[2])]

    pat = [[-1, 8], [-64, 2]]
    t_ie = do("g", [], lambda: g.iota(T.ie[:], pat, 0, 1, allow_small_or_imprecise_dtypes=True))
    t_iei = do("g", [], lambda: g.iota(T.iei[:], pat, 0, 1))
    t_ones = do("v", [], lambda: V.memset(T.ones[:], 1.0))
    t_or = do("v", [], lambda: V.memset(T.orow[0:1, :], 1.0))
    t_z = do("v", [], [lambda: V.memset(T.tw[:, R:R + 8], 0), lambda: V.memset(T.mw[:, 128:144], 0.0)])
    t_pw0 = do("s", [t_ie], lambda: A.activation(T.pw0[:], T.ie[:], ACT.Exp, bias=7 * ln2, scale=-ln2 / 8))
    t_id = do("g", [t_ones], lambda: g.affine_select(T.idb[:], T.ones[:], [[1, 128]], ALU.is_equal, 0.0, 0, -1))
    t_is = do("g", [], lambda: g.iota(T.isl[:], [[-1, 10]], 128, 1))
    t_ip = do("g", [], lambda: g.iota(T.ip[:], [[1, 16]], 0, 16))
    t_vf = [do("v", [], lambda: V.memset(T.v[:, 0:320], float(R)))]
    t_iem = do("v", [t_iei], lambda: V.tensor_scalar(T.iem[:], T.iei[:], 0xFFC7, None, ALU.bitwise_and))
    t_pm = do("v", [t_iem], lambda: V.tensor_scalar(T.pm[:], T.iem[:], 0.0, None, ALU.is_equal))

    wait("g", t_ld[0])
    rid, pid = topo.addr(hp[0], core)
    g.remote_dma(T.hs[0:128, :], T.tw[:, S7:S7 + W0], S.hsm, S.h00, pid, rid, bits(eng))

    t_lf = do("v", [t_lim], lambda: V.tensor_copy(T.limf[0:1, :], T.limi[0:1, :]))
    t_pl = do("t", [t_or, t_lf], lambda: P.matmul(T.psa[:, 0:2], T.orow[0:1, :], T.limf[0:1, :], True, True))
    t_vf.append(do("v", [], lambda: V.memset(T.v[:, 320:512], float(R))))
    t_ml = do("v", [t_x0, t_pl], [lambda: V.tensor_scalar(T.ml[:], T.x0[:], T.psa[:, 0:1], None, ALU.is_lt),
                                  lambda: V.tensor_scalar(T.mk[:], T.x0[:], T.psa[:, 1:2], None, ALU.is_gt)])
    t_pw = do("v", [t_pw0, t_pm], lambda: V.tensor_tensor(T.pw[:], T.pw0[:], T.pm[:], ALU.mult))
    t_pp = do("t", [t_ml, t_pw], [lambda: P.matmul(T.psa[:, 16:32], T.ml[:], T.pw[:], True, False),
                                  lambda: P.matmul(T.psa[:, 16:32], T.mk[:], T.pw[:], False, True)])
    t_mef = do("v", [t_mei], lambda: V.tensor_copy(T.mef[:], T.mei[:]))
    ow = T.mw[:, 16 * me:16 * me + 16]
    t_own = do("v", [t_pp], lambda: V.tensor_copy(ow, T.psa[:, 16:32]))
    wait("g", t_own)
    g.remote_dma_fused([RemoteDMATransfer(dst_ids=[dest(r) for r in peers], dma_engine_mask=bits(eng),
                                          remote_sem=S.mi, srcs=[ow], dsts=[ow for r in peers])], local_sem=S.h1)
    for k in range(2):
        wait("g", t_ld[k + 1])
        feed(k)
    wait("y", ("go1", 1))
    t_ld.append(load(C0[2], BLK))

    t_bf = do("v", [t_fk], lambda: V.tensor_scalar(T.bf[:], T.fks[:], 1.0 / 1024, 191.5 + 1.0 / 2048, ALU.mult, ALU.add))
    t_k1 = do("v", [], lambda: V.tensor_scalar(T.k1[:], T.fks[:], 1023, None, ALU.bitwise_and))
    t_kp = do("v", [], [lambda c=c: V.tensor_copy(T.kp[:, c::2], T.fks[:, 128 * c:128 * c + 128]) for c in range(2)])
    t_lk = do("v", [t_k1], lambda: V.tensor_copy(T.lk[:], T.k1[:]))
    t_ism = do("v", [t_is], lambda: V.tensor_scalar(T.ism[:], T.isl[:], 15, None, ALU.bitwise_and))
    t_ipm = do("v", [t_ip], [lambda: V.tensor_scalar(T.ipm[:], T.ip[:], 255, None, ALU.bitwise_and),
                             lambda: V.tensor_scalar(T.cgi[:], T.ip[:, 0:2], 8, None, ALU.arith_shift_right)])
    t_sl9 = do("v", [t_ism], lambda: V.tensor_scalar(T.sl9[:], T.ism[:], 0.0, None, ALU.is_equal))
    t_ct = do("v", [t_ipm], [lambda: V.tensor_scalar(T.ct[:], T.ipm[:], 769.0, None, ALU.add),
                             lambda: V.tensor_scalar(T.cg[:], T.cgi[:], -float(BLK), -float(BLK), ALU.mult, ALU.add)])

    t_pe = do("g", [], lambda: g.affine_select(T.prm[:], T.ones[:], [[-1, 16], [-16, 8]], ALU.is_equal, 0.0, 0, 1))
    t_bi0 = do("g", [], lambda: g.affine_select(T.bi0[:], T.ones[:, 0:8], [[-16, 8]], ALU.is_equal, 0.0, 0, 1))
    t_tri = do("g", [], lambda: g.affine_select(T.tri[:], T.ones[:], [[1, 128]], ALU.is_gt, 0.0, 0, -1))
    t_bi = do("g", [t_bi0], lambda: g.affine_select(T.bi[:], T.bi0[:], [[-16, 8]], ALU.not_equal, 1.0 / 256, -1, 1))
    t_f = do("g", [], [lambda: g.iota(T.f1[:], [[0, 6]], 0, 1), lambda: g.iota(T.f2[:], [[16, 6]], 0, 0)])

    t_idf = do("s", [t_id], lambda: A.activation(T.idf[:], T.idb[:], ACT.Copy))
    t_wkz = do("s", t_vf, [lambda: A.activation(T.wk[:, 0:512], T.v[:, 0:512], ACT.Copy, scale=0.0),
                           lambda: A.activation(T.wk[:, 512:776], T.v[:, 0:264], ACT.Copy, scale=0.0)])
    t_rs0 = do("s", [t_ones], lambda: A.activation(T.rs[:], T.ones[:], ACT.Copy))
    t_mt = do("t", [t_mef, t_idf], [lambda c=c, h=h: P.matmul(
        T.psm[0:16, 2 * h + c:256:4], T.mef[:, 16 * h:16 * h + 16], T.idf[:, 64 * c:64 * c + 64], True, True)
        for c in range(2) for h in range(2)])
    t_met = do("s", [t_mt], lambda: A.activation(T.met[0:16, :], T.psm[0:16, 0:256], ACT.Copy))
    t_rs = do("s", [t_rs0], lambda: A.activation(T.rs[:, 0::8], T.ones[:, 0:16], ACT.Copy, scale=0.0))
    t_bt = do("t", [t_pe, t_bf], [lambda c=c: P.matmul(
        T.psb[:, 128 * c:128 * c + 128], T.bf[:, 128 * c:128 * c + 128], T.prm[:], True, True) for c in range(2)])
    t_pbt = do("s", [t_bt], lambda: A.activation(T.pbt[:], T.psb[:, 0:256], ACT.Exp, bias=(8 - 192) * ln2, scale=ln2))
    t_sl8 = do("s", [t_sl9], lambda: A.activation(T.sl8[:], T.sl9[:, 0:8], ACT.Identity, bias=T.sl9[:, 8:9]))

    t_mr = do("y", [t_met, t_wkz] + t_vf, [lambda q=q: Y.dma_start(
        T.v[16 * q + 9:16 * q + 10, :], T.met[0:16, 32 * q:32 * q + 32]) for q in range(8)], 16)
    t_v = do("y", [t_kp, ("go2", 1)], [lambda q=q: Y.dma_start(
        T.v[16 * q:16 * q + 8, :], T.kp[:, 32 * q:32 * q + 32]) for q in range(8)], 16)
    wait("y", t_ld[3])
    a, b = C0[-1], BLK
    t_tw = do("y", [], [lambda t=t, lo=lo, hi=hi, src=src: Y.dma_start(
        T.tw[lo:hi, BLK * t + a:BLK * t + b], T.tw[src:src + hi - lo, S7 + a:S7 + b])
        for t in range(7) for lo, hi, src in ((0, 112 - 16 * t, 16 * t + 16), (112 - 16 * t, 128, 0))], 16)

    wait("t", ("mi", 7 * len(eng)), t_own, t_z, t_id)
    t_win = []
    for ps, ts, q in ((T.w0, (0, 1, 2), "s"), (T.w1, (3, 4, 5), "v"), (T.w2, (6, 7), "v")):
        t_t = do("t", [], [lambda i=i, t=t: P.transpose(ps[:, 128 * i:128 * i + 128], T.mw[:, 2 * t:2 * t + 128], T.idb[:])
                           for i, t in enumerate(ts)])
        o, n = 128 * ts[0], 128 * len(ts)
        t_win.append(do(q, [t_t], (lambda: A.activation(T.sw[:, o:o + n], ps[:, 0:n], ACT.Copy)) if q == "s"
                        else (lambda: V.tensor_copy(T.sw[:, o:o + n], ps[:, 0:n]))))

    sw = T.sw[:, 0:1024]
    wait("v", t_lk, *t_win)
    wait("s", t_lk, *t_win)
    t_gv = [do("v", [], lambda: V.tensor_copy(T.ge[:, 16 * a:16 * b], sw.indirect(T.lk[:, a:b]))) for a, b in ((0, 64), (128, 128 + VG))]
    t_gs = [do("s", [], lambda: A.activation(T.ge[:, 16 * a:16 * b], sw.indirect(T.lk[:, a:b]), ACT.Copy))
            for a, b in ((64, 128), (128 + VG, 256))]
    t_zoz = do("s", [t_gs[0]], lambda: A.activation(T.zo[:], T.ge[:, 1024:1264], ACT.Copy, scale=0.0))
    t_zo = do("s", [t_zoz, t_sl9], lambda: A.activation(T.zo[:, 112:128], T.zo[:, 0:16], ACT.Identity, bias=T.sl9[:, 9:10]))

    t_wk, t_pos, t_dis, t_pres = t_wkz, t_own, [], []
    for c in range(2):
        ps = (T.psd0, T.psd1)[c]
        o, a, e = 128 * c, 64 * c, 16 * c
        tot = T.pre[:, e + 15:e + 16]
        t_d = do("t", [t_bi, t_gv[c], t_gs[c]], [lambda q=q: P.matmul(
            ps[:, 8 * q:8 * q + 8], T.ge[:, 2048 * c + q:2048 * c + 2048:16], T.bi[:], True, True) for q in range(16)])
        t_di = do("v", [t_d, t_pbt], lambda: V.tensor_tensor(T.di[:, o:o + 128], ps[:, 0:128], T.pbt[:, o:o + 128], ALU.mult))
        t_db = do("v", [t_di], lambda: V.tensor_scalar(
            T.db[:, o:o + 128], T.di[:, o:o + 128], 15, 1, ALU.logical_shift_right, ALU.bitwise_and))
        t_o = do("v", [t_db, t_rs], lambda: V.tensor_tensor_scan(T.orr[:, o:o + 128], T.rs[:], T.db[:, o:o + 128], 0.0, ALU.mult, ALU.max))
        nm = T.orr[:, o + 7:o + 128:8]
        t_pre = do("v", [t_o, t_ones], lambda: V.tensor_tensor_scan(T.pre[:, e:e + 16], T.ones[:, 0:16], nm, 0.0, ALU.add, ALU.subtract))
        mms = [lambda: P.matmul(T.psa[:, 64 + c:65 + c], T.tri[:], tot, True, True)]
        if c == 0:
            mms.append(lambda: P.matmul(T.psa[:, 66:67], T.ones[:], tot, True, True))
        t_off = do("t", [t_tri, t_pos, t_pre], mms)
        t_zz = do("v", [t_ct], lambda: V.tensor_tensor(T.zz[:, e:e + 16], nm, T.ct[:], ALU.mult))
        t_aa = do("v", [t_zz, t_pre], lambda: V.tensor_tensor(T.aa[:, e:e + 16], T.pre[:, e:e + 16], T.zz[:, e:e + 16], ALU.add))
        t_pos = do("v", [t_aa, t_off], lambda: V.tensor_scalar(
            T.pos[:, e:e + 16], T.aa[:, e:e + 16], T.psa[:, 64 + c:65 + c], T.psa[:, 66:67] if c else 0.0, ALU.add, ALU.add))
        t_wk = do("v", [t_pos, t_wk, t_v, t_mr] + t_vf, lambda: V.tensor_copy(
            T.wk[:, 0:2048].indirect(T.pos[:, e:e + 16]), T.v[:, c::2]))
        t_dis.append(t_di)
        t_pres.append(t_pre)
    t_nn = do("t", [t_met] + t_pres, [lambda c=c: P.matmul(T.psm[:, 256:257], T.ones[:], T.pre[:, 16 * c + 15:16 * c + 16], c == 0, c == 1)
                                      for c in range(2)])
    t_n = do("v", [t_nn], lambda: V.tensor_copy(T.yt[:, 96:97], T.psm[:, 256:257]))

    t_k = do("t", [t_wk, t_sl8, t_dis[0]], [lambda c=c: P.matmul(
        T.psd0[:, c:48:6], T.wk[:, 1 + c:769:6], T.sl8[:], True, True) for c in range(6)])
    t_kx = do("v", [t_k], lambda: V.tensor_scalar(T.kx[:], T.psd0[:, 0:48], T.cg[:, 0:1], None, ALU.add))
    t_ky = do("v", [t_kx], lambda: V.tensor_scalar(T.ky[:], T.kx[:], 0x10000 + R - 1, None, ALU.bitwise_and))
    t_ks = do("v", [t_ky], lambda: V.tensor_scalar(T.ks[:], T.ky[:], float(R), None, ALU.min))

    wait("g", t_ks)
    for k, xs in enumerate(HOP2):
        n = len(eng) // len(xs)
        g.remote_dma_fused([RemoteDMATransfer(
            dst_ids=[dest(me ^ x)], dma_engine_mask=bits(eng[n * i:n * i + n]), remote_sem=S["l%d" % k],
            srcs=[T.ks[:, 6 * (me ^ x):6 * (me ^ x) + 6]], dsts=[T.lt[:, lcol(x):lcol(x) + 6]])
            for i, x in enumerate(xs)], local_sem=S.h2)

    t_me = do("t", [t_wk, t_zo, t_n], [lambda u=u: P.matmul(
        T.psm[:, 0:96], T.zo[:, 112 - 16 * u:240 - 16 * u], T.wk[:, 1 + 96 * u:97 + 96 * u], u == 0, u == 7) for u in range(8)])
    t_mey = do("s", [t_me], lambda: A.activation(T.mey[:], T.psm[:, 0:96], ACT.Copy))

    t_f1m = do("v", [t_f], lambda: V.tensor_scalar(T.f1m[:], T.f1[:], 15, None, ALU.bitwise_and))
    t_fv = do("v", [t_f1m], lambda: V.tensor_tensor(T.fv[:], T.f1m[:], T.f2[:], ALU.add))
    t_fw = do("v", [t_fv], [lambda: V.tensor_scalar(T.fw[:], T.fv[:], 1.0 / 6.0, -0.41666, ALU.mult, ALU.add),
                            lambda: V.tensor_scalar(T.fb[:], T.fv[:], 16.0, None, ALU.mult)])
    t_fa = do("v", [t_fw], lambda: V.tensor_scalar(T.fa[:], T.fw[:], -95.0, None, ALU.mult))
    t_fi = do("v", [t_fa], lambda: V.tensor_tensor(T.fi[:], T.fa[:], T.fb[:], ALU.add))
    t_fp = do("v", [t_fi], lambda: V.tensor_copy(T.fp[:], T.fi[:]))

    win = T.tw[:, 0:R + 8]
    ne = len(topo.engines(hp[0], core))
    wait("v", t_tw, t_z, *t_ld)
    wait("v", ("hw", 7 * (ne // 8) + NH * len(WP) * 3 * ne))
    for k, xs in enumerate(HOP3):
        x, n = xs[0], len(eng) // len(xs)
        landed = ("l%d" % [j for j, ys in enumerate(HOP2) if x in ys][0], len(eng))
        wait("g", do("v", [landed], lambda: V.tensor_copy(
            T.od[:, 96 * x:96 * (x + len(xs))], win.indirect(T.lt[:, lcol(x):lcol(x) + 6 * len(xs)]))))
        g.remote_dma_fused([RemoteDMATransfer(
            dst_ids=[dest(me ^ x)], dma_engine_mask=bits(eng[n * i:n * i + n]), remote_sem=S["d%d" % k],
            srcs=[T.od[:, 96 * x:96 * x + 96]], dsts=[T.ld[:, 96 * x:96 * x + 96]]) for i, x in enumerate(xs)], local_sem=S.h3)
    t_oo = do("v", [t_ks], lambda: V.tensor_copy(T.ld[:, 0:96], win.indirect(T.ks[:, 6 * me:6 * me + 6])))

    fp = T.fp[:, 0:6]
    t_y = do("v", [t_oo, t_fp, t_mey], lambda: V.tensor_tensor(T.acc[:, 0:96], T.ld[:, 0:96].indirect(fp), T.mey[:], ALU.add))
    for k, xs in enumerate(HOP3):
        src = T.ld[:, 96 * xs[0]:96 * xs[0] + 96]
        wait("v", ("d%d" % k, len(eng)))
        if len(xs) == 2:
            pair = T.od[:, 0:96] if k % 2 else T.b1[:, 0:96]
            wait("v", do("v", [], lambda: V.tensor_tensor(pair, src, T.ld[:, 96 * xs[1]:96 * xs[1] + 96], ALU.add)))
            src = pair
        out = T.yt[:, 0:96] if k == len(HOP3) - 1 else T.acc[:, 96 * k + 96:96 * k + 192]
        t_y = do("v", [t_y], lambda: V.tensor_tensor(out, src.indirect(fp), T.acc[:, 96 * k:96 * k + 96], ALU.add))
    done = []
    for q, us in (("y", range(0, 4)), ("s", range(4, 8))):
        done.append(do(q, [t_y, t_n], [lambda u=u: Q[q].dma_start(
            T.y[:, 96 * u:96 * u + (97 if u == 7 else 96)], T.yt[16 * u:16 * u + 16, 0:97 if u == 7 else 96]) for u in us], 16))
    wait("y", *done)
    wait("g", ("h1", len(eng)), ("h3", len(HOP3) * len(eng)), ("h2", len(HOP2) * len(eng)), ("h0", len(WP) * sum(len(x) for x in fe)), ("h00", len(eng)))
    waited = {name for _, name in seen}
    wait("g", *[(n, t) for n, t in total.items() if n not in waited])
